import numpy as np
import ml_dtypes


def mxq(x, axis, fmt="e4m3"):
    dtype, down = {"e4m3": (ml_dtypes.float8_e4m3fn, 7), "e5m2": (ml_dtypes.float8_e5m2, 14)}[fmt]
    v = np.moveaxis(np.asarray(x, np.float32).astype(ml_dtypes.bfloat16).astype(np.float64), axis, -1)
    blocks = v.reshape(v.shape[:-1] + (-1, 32))
    amax = np.abs(blocks).max(-1, keepdims=True)
    byte = np.maximum(np.where(amax > 0, np.frexp(amax)[1] - 1 + 127, 0) - down, 1)
    scale = np.exp2(byte - 127.0)
    codes = (blocks / scale).astype(np.float32).astype(dtype).astype(np.float64)
    return np.moveaxis((codes * scale).reshape(v.shape), -1, axis)


WIDE = False


def mx_kscale(k):
    if not WIDE:
        return np.ones(k)
    levels = np.array([10, -10, 5, -5, 0])
    if k % 512:
        return np.exp2(np.random.permutation(np.resize(levels, k // 32))).repeat(32)
    a = np.empty((k // 512, 16))
    for p in range(k // 512):
        a[p, :8] = np.random.permutation(np.resize(levels, 8))
        for g in range(8):
            far = levels[np.abs(levels - a[p, g]) >= 10]
            a[p, g + 8] = far[np.random.randint(len(far))]
    return np.exp2(a.ravel()).repeat(32)


def f64(x):
    return np.asarray(x).astype(np.float64)


def striped(idx):
    return np.tile(idx.reshape(-1, 16).T, (8, 1)).astype(np.uint16)


def unstriped(offs):
    return offs[:16].T.reshape(-1).astype(np.int64)


E2M1 = np.array([0.0, 0.5, 1.0, 1.5, 2.0, 3.0, 4.0, 6.0, -0.0, -0.5, -1.0, -1.5, -2.0, -3.0, -4.0, -6.0])


def pack_weight(w, fmt):
    k, n = w.shape
    w = f64(np.asarray(w, np.float32).astype(ml_dtypes.bfloat16)).reshape(k // 32, 32, n)
    amax = np.abs(w).max(1)
    if fmt == "e4m3":
        byte = np.frexp(amax)[1] - 1 + 127 - 7
    else:
        mant, ex = np.frexp(amax / 6.0)
        byte = np.where(mant > 0.5, ex, ex - 1) + 127
    byte = np.clip(np.where(amax > 0, byte, 1), 1, 254)
    scaled = (w * np.exp2(127.0 - byte)[:, None, :]).reshape(k, n).astype(np.float32)
    by_word = np.ascontiguousarray(scaled.reshape(k // 512, 128, 4, n).transpose(0, 1, 3, 2))
    if fmt == "e4m3":
        words = by_word.astype(ml_dtypes.float8_e4m3fn).view(np.uint8)
    else:
        c = by_word.astype(ml_dtypes.float4_e2m1fn).view(np.uint8) & 0xF
        words = (c[..., 0::2] | (c[..., 1::2] << 4)).reshape(k // 512, 128, 2 * n)
    return np.ascontiguousarray(words), np.ascontiguousarray(byte.astype(np.uint8).reshape(k // 512, 16, n))


def unpack_weight(words, scales, fmt):
    g, _, n = scales.shape
    words = np.ascontiguousarray(words).reshape(g, 128, n, -1)
    if fmt == "e4m3":
        vals = words.view(ml_dtypes.float8_e4m3fn).astype(np.float64)
    else:
        nib = np.empty((g, 128, n, 4), np.uint8)
        nib[..., 0::2] = words & 0xF
        nib[..., 1::2] = words >> 4
        vals = E2M1[nib]
    vals = vals * np.repeat(np.exp2(scales.astype(np.float64) - 127.0), 8, axis=1)[..., None]
    return vals.transpose(0, 1, 3, 2).reshape(g * 512, n)


def gelu(v):
    return 0.5 * v * (1.0 + np.tanh(np.sqrt(2.0 / np.pi) * (v + 0.044715 * v**3)))


def bf(x):
    return np.asarray(x, np.float32).astype(ml_dtypes.bfloat16)


def planes(Y):
    n, m = Y.shape
    b = f64(bf(Y)).reshape(n // 32, 32, m)
    amax = np.abs(b).max(1)
    byte = np.clip(np.where(amax > 0, np.frexp(amax)[1] - 1 + 127 - 7, 1), 1, 254)
    codes = (b * np.exp2(127.0 - byte)[:, None, :]).reshape(n, m).astype(np.float32).astype(ml_dtypes.float8_e4m3fn).view(np.uint8)
    words = codes.reshape(n // 512, 128, 4, m).transpose(0, 1, 3, 2)
    return np.ascontiguousarray(words), np.ascontiguousarray(byte.astype(np.uint8).reshape(n // 512, 16, m))


T, S, K, M, H, N = 2048, 1024, 1024, 512, 1024, 512

def setup_inputs():
    n = np.random.standard_normal
    s = mx_kscale(K)[:, None]
    s2 = mx_kscale(M)[:, None]
    u = mx_kscale(H)[:, None]
    tab_words, tab_scales = pack_weight(n((K, T)) * s, "e4m3")
    wm4_words, wm4_scales = pack_weight(n((M, H)) / np.sqrt(M) / s2 * u.T, "e2m1")
    return {
        "tab_words": tab_words, "tab_scales": tab_scales,
        "offs": striped(np.random.permutation(T)[:S]),
        "w1": (n((K, H)) / np.sqrt(K) / s * u.T).astype(np.float32),
        "media": (n((M, S)) * s2).astype(np.float32),
        "wm4_words": wm4_words, "wm4_scales": wm4_scales,
        "w3": (n((H, N)) / np.sqrt(H) / u).astype(np.float32),
        "goal": np.exp(0.8 * n(N)).astype(np.float32),
        "gT": (0.5 * n((N, T)) * np.exp(0.8 * n((N, 1)))).astype(np.float32),
    }

def reference(tab_words, tab_scales, offs, w1, media, wm4_words, wm4_scales, w3, goal, gT):
    v = unpack_weight(tab_words, tab_scales, "e4m3")[:, unstriped(offs)]
    a = mxq(f64(w1), 0, "e4m3").T @ v
    wm4 = unpack_weight(wm4_words, wm4_scales, "e2m1")
    b = wm4.T @ mxq(f64(media), 0, "e4m3")
    h = np.maximum(a, b)
    e = mxq(f64(w3), 0, "e4m3").T @ mxq(h, 0, "e4m3")
    blend = 1.0 / (1.0 + np.exp(-e))
    g = f64(gT)[:, unstriped(offs)]
    new = f64(goal)[:, None] * blend * (1.0 - g)
    y = f64(gT).copy()
    y[:, unstriped(offs)] = new
    words, scales = planes(y)
    return y, words, scales

@@ -1,0 +1,296 @@
+from contextlib import ExitStack
+
+import concourse.mybir as mybir
+
+T, S, K, M, H, N = 2048, 1024, 1024, 512, 1024, 512
+FLOPS = 2 * S * H * (K + M + N)
+
+F32 = mybir.dt.float32
+BF16 = mybir.dt.bfloat16
+I32 = mybir.dt.int32
+U32 = mybir.dt.uint32
+U16 = mybir.dt.uint16
+U8 = mybir.dt.uint8
+FP8X4 = mybir.dt.float8_e4m3fn_x4
+FP4X4 = mybir.dt.float4_e2m1fn_x4
+ACT = mybir.ActivationFunctionType
+ALU = mybir.AluOpType
+
+P = 128
+PACK = 4
+W = 512
+B_RING = 10
+JB = 128
+
+
+def tile_list_vaccine_uptake_step_kernel(
+    tc, tab_words, tab_scales, offs, w1, media, wm4_words, wm4_scales, w3, goal, gT, out_0, out_1, out_2
+):
+    nc = tc.nc
+    with ExitStack() as ctx:
+        keep = ctx.enter_context(tc.tile_pool(name="keep", bufs=1))
+        ring = ctx.enter_context(tc.tile_pool(name="ring", bufs=1))
+        psum = ctx.enter_context(tc.psum_pool(name="psum", bufs=1))
+
+        def held(shape, dtype, name, tag=""):
+            return keep.tile(shape, dtype, name=name, tag=tag or name, align_bytes=64)
+
+        offsets = keep.tile([P, S // 16], U16, name="offsets")
+        nc.sync.dma_start(offsets[:], offs)
+
+        tab_plane = held([P, T], U8, "tab_plane")
+        nc.vector.memset(tab_plane[:].bitcast(I32), 0)
+        wm_plane_raw = held([P, H], U8, "wm_plane_raw")
+        nc.vector.memset(wm_plane_raw[:].bitcast(I32), 0)
+
+        def load_table(a):
+            tile = held([P, T], I32, f"table{a}")
+            nc.sync.dma_start(tile[:], tab_words[a].rearrange("p t i -> p (t i)").bitcast(I32))
+            return tile
+
+        def load_rows(src, name):
+            raw = held([P, PACK, W], F32, name)
+            nc.sync.dma_start(raw[:], src.rearrange("(p j) c -> p j c", j=PACK))
+            return raw
+
+        def load_w1(a, g):
+            return load_rows(w1[W * a : W * (a + 1), W * g : W * (g + 1)], f"w1_raw{a}{g}")
+
+        def load_w3(g):
+            raw = held([P, PACK, W], F32, f"w3_raw{g}")
+            rows = w3[W * g : W * (g + 1), :].rearrange("(b t i) n -> t b i n", t=PACK, i=4)
+            for t in range(PACK):
+                nc.sync.dma_start(raw[:, t, :], rows[t])
+            return raw
+
+        def load_page(t):
+            page = held([P, T], F32, f"page{t}")
+            nc.sync.dma_start(page[:], gT.rearrange("(p t) c -> t p c", t=PACK)[t])
+            return page
+
+        table, w1_raw, media_raw, w3_raw, page = {}, {}, {}, {}, {}
+        tab_rows = held([P, T // 4], I32, "tab_rows")
+        for q in range(4):
+            nc.sync.dma_start(tab_rows[32 * q : 32 * q + 8, :], tab_scales[:, 4 * q : 4 * q + 4, :].bitcast(I32))
+        for q in range(4):
+            nc.vector.tensor_copy(tab_plane[32 * q : 32 * q + 8, :].bitcast(I32), tab_rows[32 * q : 32 * q + 8, :])
+        media_raw[0] = load_rows(media[:, 0:W], "media_raw0")
+        wm_raw = held([P, H // 2], I32, "wm_raw")
+        nc.sync.dma_start(wm_raw[:], wm4_words[0].bitcast(I32))
+        table[0] = load_table(0)
+        for q in range(4):
+            nc.sync.dma_start(
+                wm_plane_raw[32 * q : 32 * q + 4, :].bitcast(I32), wm4_scales[0, 4 * q : 4 * q + 4, :].bitcast(I32)
+            )
+        table[1] = load_table(1)
+        w1_raw[0, 0] = load_w1(0, 0)
+        w1_raw[1, 0] = load_w1(1, 0)
+        page[0] = load_page(0)
+        media_raw[1] = load_rows(media[:, W : 2 * W], "media_raw1")
+        w1_raw[0, 1] = load_w1(0, 1)
+        w1_raw[1, 1] = load_w1(1, 1)
+        page[1] = load_page(1)
+        goal_sb = held([P, PACK], F32, "goal_sb")
+        nc.sync.dma_start(goal_sb[:], goal.rearrange("(p t) -> p t", t=PACK))
+        w3_raw[0] = load_w3(0)
+        w3_raw[1] = load_w3(1)
+        page[2] = load_page(2)
+        page[3] = load_page(3)
+
+        warm = held([P, 8], F32, "warm")
+        nc.gpsimd.memset(warm[:], 0.0)
+        nc.scalar.activation(warm[:], warm[:], ACT.Sigmoid)
+        neg_goal = held([P, PACK], F32, "neg_goal")
+        nc.scalar.mul(neg_goal[:], goal_sb[:], -1.0)
+
+        def copy_on(engine, out, in_):
+            if engine == "vector":
+                nc.vector.tensor_copy(out, in_)
+            else:
+                nc.scalar.copy(out, in_)
+
+        def quantize(grouped, name):
+            codes = held([P, W], U32, name + "_codes")
+            plane = held([P, W], U8, name + "_plane")
+            nc.vector.quantize_mx(out=codes[:].bitcast(FP8X4), scales=plane[:], in_=grouped[:])
+            return codes, plane
+
+        def stage_tile(name):
+            return ring.tile([P, PACK * W], BF16, name=name, tag="stage", bufs=3, align_bytes=64)
+
+        def prep_w1(a, g, engine):
+            grouped = held([P, PACK * W], BF16, "w1_bf11") if (a, g) == (1, 1) else stage_tile(f"w1_bf{a}{g}")
+            copy_on(
+                engine,
+                grouped[:].rearrange("p (t b i j) -> p b t j i", t=4, i=4, j=4),
+                w1_raw[a, g][:].rearrange("p j (b t i) -> p b t j i", t=4, i=4),
+            )
+            return quantize(grouped, f"w1_{a}{g}")
+
+        def prep_media(half, engine):
+            grouped = held([P, PACK * W], BF16, "media_bf0") if half == 0 else stage_tile("media_bf1")
+            copy_on(
+                engine,
+                grouped[:].rearrange("p (c i j) -> p c j i", i=4, j=4),
+                media_raw[half][:].rearrange("p j (c i) -> p c j i", i=4),
+            )
+            return quantize(grouped, f"media_{half}")
+
+        def prep_w3(g, engine):
+            grouped = stage_tile(f"w3_bf{g}")
+            copy_on(
+                engine,
+                grouped[:].rearrange("p (t m j) -> p m j t", t=4, j=4),
+                w3_raw[g][:].rearrange("p j (m t) -> p m j t", t=4),
+            )
+            return quantize(grouped, f"w3_{g}")
+
+        def gather_words(a):
+            picked = held([P, S], U32, f"picked{a}", tag=f"media_bf0" if a == 0 else "")
+            nc.vector.tensor_copy(picked[:], table[a][:].bitcast(U32).indirect(offsets[:]))
+            return picked
+
+        def gather_state(t):
+            state[t] = held([P, S], F32, f"state{t}", tag=state_tag[t])
+            nc.vector.tensor_copy(state[t][:], page[t][:].indirect(offsets[:]))
+
+        def make_factor(t):
+            nc.scalar.activation(
+                factor[t][:],
+                state[t][:],
+                ACT.Identity,
+                bias=goal_sb[:, t : t + 1],
+                scale=neg_goal[:, t : t + 1],
+            )
+
+        state_tag = ["state0", "w1_bf11", "h_bf11", "h_bf10"]
+        picked, w1_q, media_q, w3_q, h_q, state = {}, {}, {}, {}, {}, {}
+
+        b_sb = {}
+
+        def make_b(g, half):
+            for jb in range(W // JB):
+                local = slice(JB * jb, JB * (jb + 1))
+                b_bank = psum.tile([P, PACK, JB], F32, name=f"b_bank{g}{half}{jb}", tag="b_bank", bufs=3)
+                for t in range(PACK):
+                    r0 = W * g + P * t
+                    nc.tensor.matmul_mx(
+                        out=b_bank[:, t, :],
+                        lhsT=wm_codes[:].bitcast(U8)[:, 2 * r0 : 2 * (r0 + P)].bitcast(FP4X4),
+                        lhsT_scale=wm_plane[:, r0 : r0 + P],
+                        rhs=media_q[half][0][:, local].bitcast(FP8X4),
+                        rhs_scale=media_q[half][1][:, local],
+                        start=True,
+                        stop=True,
+                    )
+                b_sb[g, half, jb] = ring.tile([P, JB, PACK], F32, name=f"b_sb{g}{half}{jb}", tag="b_sb", bufs=B_RING)
+                nc.scalar.copy(b_sb[g, half, jb][:], b_bank[:].rearrange("p t n -> p n t"))
+
+        def make_h(g, half):
+            grouped = held([P, PACK * W], BF16, f"h_bf{g}{half}", tag=f"h_bf1{half}")
+            for jb in range(W // JB):
+                cols = slice(W * half + JB * jb, W * half + JB * (jb + 1))
+                a_bank = psum.tile([P, PACK, JB], F32, name=f"a_bank{g}{half}{jb}", tag="a_bank", bufs=5)
+                for t in range(PACK):
+                    for a in range(2):
+                        nc.tensor.matmul_mx(
+                            out=a_bank[:, t, :],
+                            lhsT=w1_q[a, g][0][:, P * t : P * (t + 1)].bitcast(FP8X4),
+                            lhsT_scale=w1_q[a, g][1][:, P * t : P * (t + 1)],
+                            rhs=picked[a][:, cols].bitcast(FP8X4),
+                            rhs_scale=picked_plane[4 * a : P, cols],
+                            start=(a == 0),
+                            stop=(a == 1),
+                        )
+                nc.vector.tensor_tensor(
+                    grouped[:, PACK * JB * jb : PACK * JB * (jb + 1)].rearrange("p (n t) -> p n t", t=PACK),
+                    a_bank[:].rearrange("p t n -> p n t"),
+                    b_sb[g, half, jb][:],
+                    ALU.max,
+                )
+            h_q[g, half] = quantize(grouped, f"h_{g}{half}")
+
+        picked_plane = held([P, S], U8, "picked_plane")
+        nc.vector.tensor_copy(picked_plane[:], tab_plane[:].indirect(offsets[:]))
+        wm_codes = held([P, H // 2], I32, "wm_codes")
+        nc.vector.tensor_copy(
+            wm_codes[:].rearrange("p (g t b w) -> p g b t w", g=2, t=4, w=2),
+            wm_raw[:].rearrange("p (g b t w) -> p g b t w", g=2, t=4, w=2),
+        )
+        wm_plane = held([P, H], U8, "wm_plane")
+        nc.vector.tensor_copy(
+            wm_plane[:].bitcast(I32).rearrange("p (g t b) -> p g b t", g=2, t=4),
+            wm_plane_raw[:].bitcast(I32).rearrange("p (g b t) -> p g b t", g=2, t=4),
+        )
+        media_q[0] = prep_media(0, "scalar")
+        picked[0] = gather_words(0)
+        picked[1] = gather_words(1)
+        make_b(0, 0)
+        w1_q[0, 0] = prep_w1(0, 0, "vector")
+        w1_q[1, 0] = prep_w1(1, 0, "vector")
+        make_b(1, 0)
+        make_h(0, 0)
+        media_q[1] = prep_media(1, "scalar")
+        w1_q[0, 1] = prep_w1(0, 1, "scalar")
+        make_b(0, 1)
+        make_h(0, 1)
+        w1_q[1, 1] = prep_w1(1, 1, "scalar")
+        make_b(1, 1)
+        w3_q[0] = prep_w3(0, "scalar")
+        w3_q[1] = prep_w3(1, "scalar")
+        make_h(1, 0)
+        make_h(1, 1)
+
+        reuse = ["w1_raw00", "w1_raw10", "w1_raw01", "w1_raw11"]
+        blend = [held([P, S], F32, f"blend{t}", tag=reuse[t]) for t in range(PACK)]
+        factor_tag = ["w3_raw0", "w3_raw1", "h_11_codes", "h_01_codes"]
+        factor = [held([P, S], F32, f"factor{t}", tag=factor_tag[t]) for t in range(PACK)]
+        for half in range(2):
+            for t in range(PACK):
+                e_bank = psum.tile([P, W], F32, name=f"e_bank{t}{half}", tag="b_bank", bufs=3)
+                for g in range(2):
+                    nc.tensor.matmul_mx(
+                        out=e_bank[:],
+                        lhsT=w3_q[g][0][:, P * t : P * (t + 1)].bitcast(FP8X4),
+                        lhsT_scale=w3_q[g][1][:, P * t : P * (t + 1)],
+                        rhs=h_q[g, half][0][:].bitcast(FP8X4),
+                        rhs_scale=h_q[g, half][1][:],
+                        start=(g == 0),
+                        stop=(g == 1),
+                    )
+                nc.scalar.activation(blend[t][:, W * half : W * (half + 1)], e_bank[:], ACT.Sigmoid)
+        for t in range(PACK):
+            gather_state(t)
+            make_factor(t)
+
+        half_t = T // 2
+        y_bf = [held([P, half_t, PACK], BF16, f"y_bf{c}", tag=state_tag[2 + c]) for c in range(2)]
+        y_rows = out_0.rearrange("(p t) c -> t p c", t=PACK)
+        for t in range(PACK):
+            nc.vector.tensor_tensor(page[t][:].indirect(offsets[:]), blend[t][:], factor[t][:], ALU.mult)
+            nc.sync.dma_start(y_rows[t], page[t][:])
+            if t < PACK - 1:
+                for c in range(2):
+                    piece = page[t][:, half_t * c : half_t * (c + 1)]
+                    if t == PACK - 2 and c == 0:
+                        nc.scalar.copy(y_bf[c][:, :, t : t + 2], piece.unsqueeze(2).to_broadcast([P, half_t, 2]))
+                    else:
+                        nc.scalar.copy(y_bf[c][:, :, t], piece)
+        last = PACK - 1
+        y_plane = held([P, T], U8, "y_plane")
+        y_words = out_1[0].rearrange("p m t -> p (m t)").bitcast(I32)
+        nc.vector.tensor_copy(y_bf[0][:, :, last], page[last][:, 0:half_t])
+        for x in range(0, half_t, W):
+            nc.scalar.copy(y_bf[1][:, x : x + W, last], page[last][:, half_t + x : half_t + x + W])
+        for x in range(0, T, W):
+            y_codes = held([P, W], I32, f"y_codes{x}")
+            lo = x % half_t
+            nc.vector.quantize_mx(
+                out=y_codes[:].bitcast(FP8X4),
+                scales=y_plane[:, x : x + W],
+                in_=y_bf[x // half_t][:, lo : lo + W, :].rearrange("p c t -> p (c t)"),
+            )
+            nc.sync.dma_start(y_words[:, x : x + W], y_codes[:])
+        for q in range(4):
+            queue = nc.sync if q % 2 == 0 else nc.scalar
+            queue.dma_start(out_2[0, 4 * q : 4 * q + 4, :].bitcast(I32), y_plane[32 * q : 32 * q + 4, :].bitcast(I32))

@@ -39,9 +39,9 @@ def tile_list_vaccine_uptake_step_kernel(
         nc.sync.dma_start(offsets[:], offs)
 
         tab_plane = held([P, T], U8, "tab_plane")
-        nc.vector.memset(tab_plane[:].bitcast(I32), 0)
+        nc.gpsimd.memset(tab_plane[:].bitcast(I32), 0)
         wm_plane_raw = held([P, H], U8, "wm_plane_raw")
-        nc.vector.memset(wm_plane_raw[:].bitcast(I32), 0)
+        nc.gpsimd.memset(wm_plane_raw[:].bitcast(I32), 0)
 
         def load_table(a):
             tile = held([P, T], I32, f"table{a}")
@@ -75,21 +75,21 @@ def tile_list_vaccine_uptake_step_kernel(
         for q in range(4):
             nc.vector.tensor_copy(tab_plane[32 * q : 32 * q + 8, :].bitcast(I32), tab_rows[32 * q : 32 * q + 8, :])
         media_raw[0] = load_rows(media[:, 0:W], "media_raw0")
+        table[0] = load_table(0)
         wm_raw = held([P, H // 2], I32, "wm_raw")
         nc.sync.dma_start(wm_raw[:], wm4_words[0].bitcast(I32))
-        table[0] = load_table(0)
         for q in range(4):
             nc.sync.dma_start(
                 wm_plane_raw[32 * q : 32 * q + 4, :].bitcast(I32), wm4_scales[0, 4 * q : 4 * q + 4, :].bitcast(I32)
             )
-        table[1] = load_table(1)
         w1_raw[0, 0] = load_w1(0, 0)
+        table[1] = load_table(1)
         w1_raw[1, 0] = load_w1(1, 0)
         page[0] = load_page(0)
         media_raw[1] = load_rows(media[:, W : 2 * W], "media_raw1")
         w1_raw[0, 1] = load_w1(0, 1)
-        w1_raw[1, 1] = load_w1(1, 1)
         page[1] = load_page(1)
+        w1_raw[1, 1] = load_w1(1, 1)
         goal_sb = held([P, PACK], F32, "goal_sb")
         nc.sync.dma_start(goal_sb[:], goal.rearrange("(p t) -> p t", t=PACK))
         w3_raw[0] = load_w3(0)
@@ -97,9 +97,6 @@ def tile_list_vaccine_uptake_step_kernel(
         page[2] = load_page(2)
         page[3] = load_page(3)
 
-        warm = held([P, 8], F32, "warm")
-        nc.gpsimd.memset(warm[:], 0.0)
-        nc.scalar.activation(warm[:], warm[:], ACT.Sigmoid)
         neg_goal = held([P, PACK], F32, "neg_goal")
         nc.scalar.mul(neg_goal[:], goal_sb[:], -1.0)
 
@@ -109,14 +106,14 @@ def tile_list_vaccine_uptake_step_kernel(
             else:
                 nc.scalar.copy(out, in_)
 
-        def quantize(grouped, name):
-            codes = held([P, W], U32, name + "_codes")
+        def quantize(grouped, name, tag=""):
+            codes = held([P, W], U32, name + "_codes", tag=tag)
             plane = held([P, W], U8, name + "_plane")
             nc.vector.quantize_mx(out=codes[:].bitcast(FP8X4), scales=plane[:], in_=grouped[:])
             return codes, plane
 
         def stage_tile(name):
-            return ring.tile([P, PACK * W], BF16, name=name, tag="stage", bufs=3, align_bytes=64)
+            return ring.tile([P, PACK * W], BF16, name=name, tag="stage", bufs=2, align_bytes=64)
 
         def prep_w1(a, g, engine):
             grouped = held([P, PACK * W], BF16, "w1_bf11") if (a, g) == (1, 1) else stage_tile(f"w1_bf{a}{g}")
@@ -128,7 +125,7 @@ def tile_list_vaccine_uptake_step_kernel(
             return quantize(grouped, f"w1_{a}{g}")
 
         def prep_media(half, engine):
-            grouped = held([P, PACK * W], BF16, "media_bf0") if half == 0 else stage_tile("media_bf1")
+            grouped = held([P, PACK * W], BF16, "media_bf1") if half == 1 else stage_tile("media_bf0")
             copy_on(
                 engine,
                 grouped[:].rearrange("p (c i j) -> p c j i", i=4, j=4),
@@ -137,7 +134,7 @@ def tile_list_vaccine_uptake_step_kernel(
             return quantize(grouped, f"media_{half}")
 
         def prep_w3(g, engine):
-            grouped = stage_tile(f"w3_bf{g}")
+            grouped = held([P, PACK * W], BF16, "w3_bf1") if g == 1 else stage_tile("w3_bf0")
             copy_on(
                 engine,
                 grouped[:].rearrange("p (t m j) -> p m j t", t=4, j=4),
@@ -146,7 +143,7 @@ def tile_list_vaccine_uptake_step_kernel(
             return quantize(grouped, f"w3_{g}")
 
         def gather_words(a):
-            picked = held([P, S], U32, f"picked{a}", tag=f"media_bf0" if a == 0 else "")
+            picked = held([P, S], U32, f"picked{a}")
             nc.vector.tensor_copy(picked[:], table[a][:].bitcast(U32).indirect(offsets[:]))
             return picked
 
@@ -156,14 +153,16 @@ def tile_list_vaccine_uptake_step_kernel(
 
         def make_factor(t):
             nc.scalar.activation(
-                factor[t][:],
+                factor[t],
                 state[t][:],
                 ACT.Identity,
                 bias=goal_sb[:, t : t + 1],
                 scale=neg_goal[:, t : t + 1],
             )
 
-        state_tag = ["state0", "w1_bf11", "h_bf11", "h_bf10"]
+        state_tag = ["state0", "state1", "h_bf11", "w1_raw00"]
+        h_tag = {(0, 0): "media_bf1", (0, 1): "w1_bf11", (1, 0): "", (1, 1): "w3_bf1"}
+        h_bf = {}
         picked, w1_q, media_q, w3_q, h_q, state = {}, {}, {}, {}, {}, {}
 
         b_sb = {}
@@ -187,7 +186,8 @@ def tile_list_vaccine_uptake_step_kernel(
                 nc.scalar.copy(b_sb[g, half, jb][:], b_bank[:].rearrange("p t n -> p n t"))
 
         def make_h(g, half):
-            grouped = held([P, PACK * W], BF16, f"h_bf{g}{half}", tag=f"h_bf1{half}")
+            grouped = held([P, PACK * W], BF16, f"h_bf{g}{half}", tag=f"table{half}" if g == 0 else "")
+            h_bf[g, half] = grouped
             for jb in range(W // JB):
                 cols = slice(W * half + JB * jb, W * half + JB * (jb + 1))
                 a_bank = psum.tile([P, PACK, JB], F32, name=f"a_bank{g}{half}{jb}", tag="a_bank", bufs=5)
@@ -208,10 +208,14 @@ def tile_list_vaccine_uptake_step_kernel(
                     b_sb[g, half, jb][:],
                     ALU.max,
                 )
-            h_q[g, half] = quantize(grouped, f"h_{g}{half}")
+
+        def quantize_h(g, half):
+            h_q[g, half] = quantize(h_bf[g, half], f"h_{g}{half}", tag=h_tag[g, half])
 
         picked_plane = held([P, S], U8, "picked_plane")
         nc.vector.tensor_copy(picked_plane[:], tab_plane[:].indirect(offsets[:]))
+        media_q[0] = prep_media(0, "scalar")
+        picked[0] = gather_words(0)
         wm_codes = held([P, H // 2], I32, "wm_codes")
         nc.vector.tensor_copy(
             wm_codes[:].rearrange("p (g t b w) -> p g b t w", g=2, t=4, w=2),
@@ -222,31 +226,36 @@ def tile_list_vaccine_uptake_step_kernel(
             wm_plane[:].bitcast(I32).rearrange("p (g t b) -> p g b t", g=2, t=4),
             wm_plane_raw[:].bitcast(I32).rearrange("p (g b t) -> p g b t", g=2, t=4),
         )
-        media_q[0] = prep_media(0, "scalar")
-        picked[0] = gather_words(0)
-        picked[1] = gather_words(1)
         make_b(0, 0)
         w1_q[0, 0] = prep_w1(0, 0, "vector")
+        picked[1] = gather_words(1)
         w1_q[1, 0] = prep_w1(1, 0, "vector")
         make_b(1, 0)
+        gather_state(0)
         make_h(0, 0)
         media_q[1] = prep_media(1, "scalar")
+        quantize_h(0, 0)
         w1_q[0, 1] = prep_w1(0, 1, "scalar")
+        gather_state(1)
         make_b(0, 1)
         make_h(0, 1)
         w1_q[1, 1] = prep_w1(1, 1, "scalar")
-        make_b(1, 1)
+        quantize_h(0, 1)
         w3_q[0] = prep_w3(0, "scalar")
-        w3_q[1] = prep_w3(1, "scalar")
+        make_b(1, 1)
         make_h(1, 0)
         make_h(1, 1)
+        w3_q[1] = prep_w3(1, "scalar")
+        quantize_h(1, 0)
+        quantize_h(1, 1)
 
         reuse = ["w1_raw00", "w1_raw10", "w1_raw01", "w1_raw11"]
         blend = [held([P, S], F32, f"blend{t}", tag=reuse[t]) for t in range(PACK)]
-        factor_tag = ["w3_raw0", "w3_raw1", "h_11_codes", "h_01_codes"]
-        factor = [held([P, S], F32, f"factor{t}", tag=factor_tag[t]) for t in range(PACK)]
-        for half in range(2):
-            for t in range(PACK):
+        factor_pair = [held([P, 2, S], F32, f"factor_pair{u}", tag=f"w3_raw{1 - u}") for u in range(2)]
+        factor = [factor_pair[t // 2][:, t % 2, :] for t in range(PACK)]
+        make_factor(0)
+        for t in range(PACK):
+            for half in range(2):
                 e_bank = psum.tile([P, W], F32, name=f"e_bank{t}{half}", tag="b_bank", bufs=3)
                 for g in range(2):
                     nc.tensor.matmul_mx(
@@ -259,15 +268,15 @@ def tile_list_vaccine_uptake_step_kernel(
                         stop=(g == 1),
                     )
                 nc.scalar.activation(blend[t][:, W * half : W * (half + 1)], e_bank[:], ACT.Sigmoid)
-        for t in range(PACK):
-            gather_state(t)
-            make_factor(t)
+        make_factor(1)
+        gather_state(2)
+        make_factor(2)
 
         half_t = T // 2
-        y_bf = [held([P, half_t, PACK], BF16, f"y_bf{c}", tag=state_tag[2 + c]) for c in range(2)]
+        y_bf = [held([P, half_t, PACK], BF16, f"y_bf{c}", tag=["w3_bf1", "w3_1_codes"][c]) for c in range(2)]
         y_rows = out_0.rearrange("(p t) c -> t p c", t=PACK)
         for t in range(PACK):
-            nc.vector.tensor_tensor(page[t][:].indirect(offsets[:]), blend[t][:], factor[t][:], ALU.mult)
+            nc.vector.tensor_tensor(page[t][:].indirect(offsets[:]), blend[t][:], factor[t], ALU.mult)
             nc.sync.dma_start(y_rows[t], page[t][:])
             if t < PACK - 1:
                 for c in range(2):
@@ -276,10 +285,14 @@ def tile_list_vaccine_uptake_step_kernel(
                         nc.scalar.copy(y_bf[c][:, :, t : t + 2], piece.unsqueeze(2).to_broadcast([P, half_t, 2]))
                     else:
                         nc.scalar.copy(y_bf[c][:, :, t], piece)
+            if t == 1:
+                gather_state(PACK - 1)
+                make_factor(PACK - 1)
         last = PACK - 1
         y_plane = held([P, T], U8, "y_plane")
         y_words = out_1[0].rearrange("p m t -> p (m t)").bitcast(I32)
-        nc.vector.tensor_copy(y_bf[0][:, :, last], page[last][:, 0:half_t])
+        for x in range(0, half_t, W):
+            nc.vector.tensor_copy(y_bf[0][:, x : x + W, last], page[last][:, x : x + W])
         for x in range(0, half_t, W):
             nc.scalar.copy(y_bf[1][:, x : x + W, last], page[last][:, half_t + x : half_t + x + W])
         for x in range(0, T, W):

@@ -19,7 +19,7 @@ ALU = mybir.AluOpType
 P = 128
 PACK = 4
 W = 512
-B_RING = 10
+B_RING = 16
 JB = 128
 
 
@@ -82,10 +82,10 @@ def tile_list_vaccine_uptake_step_kernel(
             nc.sync.dma_start(
                 wm_plane_raw[32 * q : 32 * q + 4, :].bitcast(I32), wm4_scales[0, 4 * q : 4 * q + 4, :].bitcast(I32)
             )
-        w1_raw[0, 0] = load_w1(0, 0)
-        table[1] = load_table(1)
-        w1_raw[1, 0] = load_w1(1, 0)
         page[0] = load_page(0)
+        w1_raw[0, 0] = load_w1(0, 0)
+        w1_raw[1, 0] = load_w1(1, 0)
+        table[1] = load_table(1)
         media_raw[1] = load_rows(media[:, W : 2 * W], "media_raw1")
         w1_raw[0, 1] = load_w1(0, 1)
         page[1] = load_page(1)
@@ -97,6 +97,9 @@ def tile_list_vaccine_uptake_step_kernel(
         page[2] = load_page(2)
         page[3] = load_page(3)
 
+        warm = held([P, 8], F32, "warm")
+        nc.gpsimd.memset(warm[:], 0.0)
+        nc.scalar.activation(warm[:], warm[:], ACT.Sigmoid)
         neg_goal = held([P, PACK], F32, "neg_goal")
         nc.scalar.mul(neg_goal[:], goal_sb[:], -1.0)
 
@@ -113,15 +116,18 @@ def tile_list_vaccine_uptake_step_kernel(
             return codes, plane
 
         def stage_tile(name):
-            return ring.tile([P, PACK * W], BF16, name=name, tag="stage", bufs=2, align_bytes=64)
+            return ring.tile([P, PACK * W], BF16, name=name, tag="stage", bufs=1, align_bytes=64)
 
-        def prep_w1(a, g, engine):
-            grouped = held([P, PACK * W], BF16, "w1_bf11") if (a, g) == (1, 1) else stage_tile(f"w1_bf{a}{g}")
+        def cast_w1(a, g, engine, grouped):
             copy_on(
                 engine,
-                grouped[:].rearrange("p (t b i j) -> p b t j i", t=4, i=4, j=4),
+                grouped.rearrange("p (t b i j) -> p b t j i", t=4, i=4, j=4),
                 w1_raw[a, g][:].rearrange("p j (b t i) -> p b t j i", t=4, i=4),
             )
+
+        def prep_w1(a, g, engine):
+            grouped = held([P, PACK * W], BF16, "w1_bf11") if a == 1 else stage_tile("w1_bf01")
+            cast_w1(a, g, engine, grouped[:])
             return quantize(grouped, f"w1_{a}{g}")
 
         def prep_media(half, engine):
@@ -142,9 +148,11 @@ def tile_list_vaccine_uptake_step_kernel(
             )
             return quantize(grouped, f"w3_{g}")
 
-        def gather_words(a):
+        def gather_words(a, parts):
             picked = held([P, S], U32, f"picked{a}")
-            nc.vector.tensor_copy(picked[:], table[a][:].bitcast(U32).indirect(offsets[:]))
+            for part in range(parts):
+                lo, hi = S * part // parts, S * (part + 1) // parts
+                nc.vector.tensor_copy(picked[:, lo:hi], table[a][:].bitcast(U32).indirect(offsets[:, lo // 16 : hi // 16]))
             return picked
 
         def gather_state(t):
@@ -182,8 +190,9 @@ def tile_list_vaccine_uptake_step_kernel(
                         start=True,
                         stop=True,
                     )
-                b_sb[g, half, jb] = ring.tile([P, JB, PACK], F32, name=f"b_sb{g}{half}{jb}", tag="b_sb", bufs=B_RING)
-                nc.scalar.copy(b_sb[g, half, jb][:], b_bank[:].rearrange("p t n -> p n t"))
+                slot = ring.tile([P, JB, PACK], F32, name=f"b_sb{g}{half}{jb}", tag="b_sb", bufs=B_RING)
+                b_sb[g, half, jb] = slot[:]
+                nc.scalar.copy(b_sb[g, half, jb], b_bank[:].rearrange("p t n -> p n t"))
 
         def make_h(g, half):
             grouped = held([P, PACK * W], BF16, f"h_bf{g}{half}", tag=f"table{half}" if g == 0 else "")
@@ -191,21 +200,21 @@ def tile_list_vaccine_uptake_step_kernel(
             for jb in range(W // JB):
                 cols = slice(W * half + JB * jb, W * half + JB * (jb + 1))
                 a_bank = psum.tile([P, PACK, JB], F32, name=f"a_bank{g}{half}{jb}", tag="a_bank", bufs=5)
-                for t in range(PACK):
-                    for a in range(2):
+                for a in range(2):
+                    for t in range(PACK):
                         nc.tensor.matmul_mx(
                             out=a_bank[:, t, :],
                             lhsT=w1_q[a, g][0][:, P * t : P * (t + 1)].bitcast(FP8X4),
                             lhsT_scale=w1_q[a, g][1][:, P * t : P * (t + 1)],
                             rhs=picked[a][:, cols].bitcast(FP8X4),
                             rhs_scale=picked_plane[4 * a : P, cols],
-                            start=(a == 0),
-                            stop=(a == 1),
+                            start=(a == 0 and t == 0),
+                            stop=(a == 1 and t == PACK - 1),
                         )
                 nc.vector.tensor_tensor(
                     grouped[:, PACK * JB * jb : PACK * JB * (jb + 1)].rearrange("p (n t) -> p n t", t=PACK),
                     a_bank[:].rearrange("p t n -> p n t"),
-                    b_sb[g, half, jb][:],
+                    b_sb[g, half, jb],
                     ALU.max,
                 )
 
@@ -215,7 +224,7 @@ def tile_list_vaccine_uptake_step_kernel(
         picked_plane = held([P, S], U8, "picked_plane")
         nc.vector.tensor_copy(picked_plane[:], tab_plane[:].indirect(offsets[:]))
         media_q[0] = prep_media(0, "scalar")
-        picked[0] = gather_words(0)
+        picked[0] = gather_words(0, 1)
         wm_codes = held([P, H // 2], I32, "wm_codes")
         nc.vector.tensor_copy(
             wm_codes[:].rearrange("p (g t b w) -> p g b t w", g=2, t=4, w=2),
@@ -226,12 +235,19 @@ def tile_list_vaccine_uptake_step_kernel(
             wm_plane[:].bitcast(I32).rearrange("p (g t b) -> p g b t", g=2, t=4),
             wm_plane_raw[:].bitcast(I32).rearrange("p (g b t) -> p g b t", g=2, t=4),
         )
-        make_b(0, 0)
-        w1_q[0, 0] = prep_w1(0, 0, "vector")
-        picked[1] = gather_words(1)
-        w1_q[1, 0] = prep_w1(1, 0, "vector")
-        make_b(1, 0)
         gather_state(0)
+        w1_first = held([P, 2 * PACK * W], BF16, "w1_first")
+        cast_w1(0, 0, "vector", w1_first[:, 0 : PACK * W])
+        cast_w1(1, 0, "vector", w1_first[:, PACK * W : 2 * PACK * W])
+        make_b(0, 0)
+        first_codes = held([P, 2 * W], U32, "first_codes")
+        first_plane = held([P, 2 * W], U8, "first_plane")
+        nc.vector.quantize_mx(out=first_codes[:].bitcast(FP8X4), scales=first_plane[:], in_=w1_first[:])
+        for a in range(2):
+            w1_q[a, 0] = first_codes[:, W * a : W * (a + 1)], first_plane[:, W * a : W * (a + 1)]
+        picked[1] = gather_words(1, 2)
+        make_b(1, 0)
+
         make_h(0, 0)
         media_q[1] = prep_media(1, "scalar")
         quantize_h(0, 0)
@@ -248,6 +264,7 @@ def tile_list_vaccine_uptake_step_kernel(
         w3_q[1] = prep_w3(1, "scalar")
         quantize_h(1, 0)
         quantize_h(1, 1)
+
 
         reuse = ["w1_raw00", "w1_raw10", "w1_raw01", "w1_raw11"]
         blend = [held([P, S], F32, f"blend{t}", tag=reuse[t]) for t in range(PACK)]
@@ -289,21 +306,21 @@ def tile_list_vaccine_uptake_step_kernel(
                 gather_state(PACK - 1)
                 make_factor(PACK - 1)
         last = PACK - 1
-        y_plane = held([P, T], U8, "y_plane")
+        y_plane = held([P, T], U8, "y_plane", tag="tab_rows")
+        y_codes = held([P, T], I32, "y_codes", tag="media_raw0")
         y_words = out_1[0].rearrange("p m t -> p (m t)").bitcast(I32)
         for x in range(0, half_t, W):
             nc.vector.tensor_copy(y_bf[0][:, x : x + W, last], page[last][:, x : x + W])
         for x in range(0, half_t, W):
             nc.scalar.copy(y_bf[1][:, x : x + W, last], page[last][:, half_t + x : half_t + x + W])
         for x in range(0, T, W):
-            y_codes = held([P, W], I32, f"y_codes{x}")
             lo = x % half_t
             nc.vector.quantize_mx(
-                out=y_codes[:].bitcast(FP8X4),
+                out=y_codes[:, x : x + W].bitcast(FP8X4),
                 scales=y_plane[:, x : x + W],
                 in_=y_bf[x // half_t][:, lo : lo + W, :].rearrange("p c t -> p (c t)"),
             )
-            nc.sync.dma_start(y_words[:, x : x + W], y_codes[:])
+            nc.sync.dma_start(y_words[:, x : x + W], y_codes[:, x : x + W])
         for q in range(4):
             queue = nc.sync if q % 2 == 0 else nc.scalar
             queue.dma_start(out_2[0, 4 * q : 4 * q + 4, :].bitcast(I32), y_plane[32 * q : 32 * q + 4, :].bitcast(I32))

@@ -74,8 +74,8 @@ def tile_list_vaccine_uptake_step_kernel(
             nc.sync.dma_start(tab_rows[32 * q : 32 * q + 8, :], tab_scales[:, 4 * q : 4 * q + 4, :].bitcast(I32))
         for q in range(4):
             nc.vector.tensor_copy(tab_plane[32 * q : 32 * q + 8, :].bitcast(I32), tab_rows[32 * q : 32 * q + 8, :])
-        media_raw[0] = load_rows(media[:, 0:W], "media_raw0")
         table[0] = load_table(0)
+        media_raw[0] = load_rows(media[:, 0:W], "media_raw0")
         wm_raw = held([P, H // 2], I32, "wm_raw")
         nc.sync.dma_start(wm_raw[:], wm4_words[0].bitcast(I32))
         for q in range(4):
@@ -116,7 +116,7 @@ def tile_list_vaccine_uptake_step_kernel(
             return codes, plane
 
         def stage_tile(name):
-            return ring.tile([P, PACK * W], BF16, name=name, tag="stage", bufs=1, align_bytes=64)
+            return ring.tile([P, PACK * W], BF16, name=name, tag="stage", bufs=3, align_bytes=64)
 
         def cast_w1(a, g, engine, grouped):
             copy_on(
@@ -126,7 +126,7 @@ def tile_list_vaccine_uptake_step_kernel(
             )
 
         def prep_w1(a, g, engine):
-            grouped = held([P, PACK * W], BF16, "w1_bf11") if a == 1 else stage_tile("w1_bf01")
+            grouped = held([P, PACK * W], BF16, "w1_bf11") if (a, g) == (1, 1) else stage_tile(f"w1_bf{a}{g}")
             cast_w1(a, g, engine, grouped[:])
             return quantize(grouped, f"w1_{a}{g}")
 
@@ -178,7 +178,7 @@ def tile_list_vaccine_uptake_step_kernel(
         def make_b(g, half):
             for jb in range(W // JB):
                 local = slice(JB * jb, JB * (jb + 1))
-                b_bank = psum.tile([P, PACK, JB], F32, name=f"b_bank{g}{half}{jb}", tag="b_bank", bufs=3)
+                b_bank = psum.tile([P, PACK, JB], F32, name=f"b_bank{g}{half}{jb}", tag="b_bank", bufs=2)
                 for t in range(PACK):
                     r0 = W * g + P * t
                     nc.tensor.matmul_mx(
@@ -199,7 +199,7 @@ def tile_list_vaccine_uptake_step_kernel(
             h_bf[g, half] = grouped
             for jb in range(W // JB):
                 cols = slice(W * half + JB * jb, W * half + JB * (jb + 1))
-                a_bank = psum.tile([P, PACK, JB], F32, name=f"a_bank{g}{half}{jb}", tag="a_bank", bufs=5)
+                a_bank = psum.tile([P, PACK, JB], F32, name=f"a_bank{g}{half}{jb}", tag="a_bank", bufs=6)
                 for a in range(2):
                     for t in range(PACK):
                         nc.tensor.matmul_mx(
@@ -223,7 +223,6 @@ def tile_list_vaccine_uptake_step_kernel(
 
         picked_plane = held([P, S], U8, "picked_plane")
         nc.vector.tensor_copy(picked_plane[:], tab_plane[:].indirect(offsets[:]))
-        media_q[0] = prep_media(0, "scalar")
         picked[0] = gather_words(0, 1)
         wm_codes = held([P, H // 2], I32, "wm_codes")
         nc.vector.tensor_copy(
@@ -235,16 +234,11 @@ def tile_list_vaccine_uptake_step_kernel(
             wm_plane[:].bitcast(I32).rearrange("p (g t b) -> p g b t", g=2, t=4),
             wm_plane_raw[:].bitcast(I32).rearrange("p (g b t) -> p g b t", g=2, t=4),
         )
+        media_q[0] = prep_media(0, "scalar")
         gather_state(0)
-        w1_first = held([P, 2 * PACK * W], BF16, "w1_first")
-        cast_w1(0, 0, "vector", w1_first[:, 0 : PACK * W])
-        cast_w1(1, 0, "vector", w1_first[:, PACK * W : 2 * PACK * W])
         make_b(0, 0)
-        first_codes = held([P, 2 * W], U32, "first_codes")
-        first_plane = held([P, 2 * W], U8, "first_plane")
-        nc.vector.quantize_mx(out=first_codes[:].bitcast(FP8X4), scales=first_plane[:], in_=w1_first[:])
-        for a in range(2):
-            w1_q[a, 0] = first_codes[:, W * a : W * (a + 1)], first_plane[:, W * a : W * (a + 1)]
+        w1_q[0, 0] = prep_w1(0, 0, "vector")
+        w1_q[1, 0] = prep_w1(1, 0, "vector")
         picked[1] = gather_words(1, 2)
         make_b(1, 0)
 
@@ -273,7 +267,7 @@ def tile_list_vaccine_uptake_step_kernel(
         make_factor(0)
         for t in range(PACK):
             for half in range(2):
-                e_bank = psum.tile([P, W], F32, name=f"e_bank{t}{half}", tag="b_bank", bufs=3)
+                e_bank = psum.tile([P, W], F32, name=f"e_bank{t}{half}", tag="a_bank", bufs=6)
                 for g in range(2):
                     nc.tensor.matmul_mx(
                         out=e_bank[:],

@@ -69,19 +69,17 @@ def tile_list_vaccine_uptake_step_kernel(
             return page
 
         table, w1_raw, media_raw, w3_raw, page = {}, {}, {}, {}, {}
-        tab_rows = held([P, T // 4], I32, "tab_rows")
-        for q in range(4):
-            nc.sync.dma_start(tab_rows[32 * q : 32 * q + 8, :], tab_scales[:, 4 * q : 4 * q + 4, :].bitcast(I32))
-        for q in range(4):
-            nc.vector.tensor_copy(tab_plane[32 * q : 32 * q + 8, :].bitcast(I32), tab_rows[32 * q : 32 * q + 8, :])
         table[0] = load_table(0)
+        for q in range(4):
+            nc.sync.dma_start(
+                tab_plane[32 * q : 32 * q + 8, :].bitcast(I32), tab_scales[:, 4 * q : 4 * q + 4, :].bitcast(I32)
+            )
         media_raw[0] = load_rows(media[:, 0:W], "media_raw0")
         wm_raw = held([P, H // 2], I32, "wm_raw")
         nc.sync.dma_start(wm_raw[:], wm4_words[0].bitcast(I32))
-        for q in range(4):
-            nc.sync.dma_start(
-                wm_plane_raw[32 * q : 32 * q + 4, :].bitcast(I32), wm4_scales[0, 4 * q : 4 * q + 4, :].bitcast(I32)
-            )
+        wm_rows = wm4_scales[0].rearrange("(q r) c -> r q c", r=4)
+        for r in range(4):
+            nc.sync.dma_start(wm_plane_raw[r:P:32, :].bitcast(I32), wm_rows[r].bitcast(I32))
         page[0] = load_page(0)
         w1_raw[0, 0] = load_w1(0, 0)
         w1_raw[1, 0] = load_w1(1, 0)
@@ -90,10 +88,10 @@ def tile_list_vaccine_uptake_step_kernel(
         w1_raw[0, 1] = load_w1(0, 1)
         page[1] = load_page(1)
         w1_raw[1, 1] = load_w1(1, 1)
-        goal_sb = held([P, PACK], F32, "goal_sb")
-        nc.sync.dma_start(goal_sb[:], goal.rearrange("(p t) -> p t", t=PACK))
         w3_raw[0] = load_w3(0)
         w3_raw[1] = load_w3(1)
+        goal_sb = held([P, PACK], F32, "goal_sb")
+        nc.sync.dma_start(goal_sb[:], goal.rearrange("(p t) -> p t", t=PACK))
         page[2] = load_page(2)
         page[3] = load_page(3)
 
@@ -300,7 +298,7 @@ def tile_list_vaccine_uptake_step_kernel(
                 gather_state(PACK - 1)
                 make_factor(PACK - 1)
         last = PACK - 1
-        y_plane = held([P, T], U8, "y_plane", tag="tab_rows")
+        y_plane = held([P, T], U8, "y_plane")
         y_codes = held([P, T], I32, "y_codes", tag="media_raw0")
         y_words = out_1[0].rearrange("p m t -> p (m t)").bitcast(I32)
         for x in range(0, half_t, W):
@@ -315,6 +313,7 @@ def tile_list_vaccine_uptake_step_kernel(
                 in_=y_bf[x // half_t][:, lo : lo + W, :].rearrange("p c t -> p (c t)"),
             )
             nc.sync.dma_start(y_words[:, x : x + W], y_codes[:, x : x + W])
-        for q in range(4):
-            queue = nc.sync if q % 2 == 0 else nc.scalar
-            queue.dma_start(out_2[0, 4 * q : 4 * q + 4, :].bitcast(I32), y_plane[32 * q : 32 * q + 4, :].bitcast(I32))
+        y_scales = out_2[0].rearrange("(q r) m -> r q m", r=4)
+        for r in range(4):
+            queue = nc.sync if r % 2 == 0 else nc.scalar
+            queue.dma_start(y_scales[r].bitcast(I32), y_plane[r:P:32, :].bitcast(I32))

@@ -19,7 +19,7 @@ ALU = mybir.AluOpType
 P = 128
 PACK = 4
 W = 512
-B_RING = 16
+B_RING = 15
 JB = 128
 
 
@@ -39,7 +39,9 @@ def tile_list_vaccine_uptake_step_kernel(
         nc.sync.dma_start(offsets[:], offs)
 
         tab_plane = held([P, T], U8, "tab_plane")
-        nc.gpsimd.memset(tab_plane[:].bitcast(I32), 0)
+        nc.sync.dma_start(tab_plane[0:32, :].bitcast(I32), tab_scales.rearrange("a q t -> (a q) t").bitcast(I32))
+        nc.gpsimd.memset(tab_plane[32:64, :].bitcast(I32), 0)
+        nc.gpsimd.memset(tab_plane[64:P, :].bitcast(I32), 0)
         wm_plane_raw = held([P, H], U8, "wm_plane_raw")
         nc.gpsimd.memset(wm_plane_raw[:].bitcast(I32), 0)
 
@@ -70,20 +72,35 @@ def tile_list_vaccine_uptake_step_kernel(
 
         table, w1_raw, media_raw, w3_raw, page = {}, {}, {}, {}, {}
         table[0] = load_table(0)
-        for q in range(4):
-            nc.sync.dma_start(
-                tab_plane[32 * q : 32 * q + 8, :].bitcast(I32), tab_scales[:, 4 * q : 4 * q + 4, :].bitcast(I32)
-            )
         media_raw[0] = load_rows(media[:, 0:W], "media_raw0")
         wm_raw = held([P, H // 2], I32, "wm_raw")
         nc.sync.dma_start(wm_raw[:], wm4_words[0].bitcast(I32))
         wm_rows = wm4_scales[0].rearrange("(q r) c -> r q c", r=4)
         for r in range(4):
             nc.sync.dma_start(wm_plane_raw[r:P:32, :].bitcast(I32), wm_rows[r].bitcast(I32))
+        picked_rows = held([P, S], U8, "picked_rows")
+        nc.vector.tensor_copy(picked_rows[:], tab_plane[:].indirect(offsets[:]))
+        picked_plane = held([P, S], U8, "picked_plane")
+        nc.gpsimd.memset(picked_plane[:].bitcast(I32), 0)
+
+        def move_rows(a, q):
+            nc.sync.dma_start(
+                picked_plane[32 * q + 4 * a : 32 * q + 4 * a + 4, :].bitcast(I32),
+                picked_rows[16 * a + 4 * q : 16 * a + 4 * q + 4, :].bitcast(I32),
+            )
+
         page[0] = load_page(0)
+        move_rows(0, 0)
+        move_rows(0, 1)
         w1_raw[0, 0] = load_w1(0, 0)
+        move_rows(0, 2)
+        move_rows(0, 3)
         w1_raw[1, 0] = load_w1(1, 0)
+        move_rows(1, 0)
+        move_rows(1, 1)
         table[1] = load_table(1)
+        move_rows(1, 2)
+        move_rows(1, 3)
         media_raw[1] = load_rows(media[:, W : 2 * W], "media_raw1")
         w1_raw[0, 1] = load_w1(0, 1)
         page[1] = load_page(1)
@@ -219,8 +236,6 @@ def tile_list_vaccine_uptake_step_kernel(
         def quantize_h(g, half):
             h_q[g, half] = quantize(h_bf[g, half], f"h_{g}{half}", tag=h_tag[g, half])
 
-        picked_plane = held([P, S], U8, "picked_plane")
-        nc.vector.tensor_copy(picked_plane[:], tab_plane[:].indirect(offsets[:]))
         picked[0] = gather_words(0, 1)
         wm_codes = held([P, H // 2], I32, "wm_codes")
         nc.vector.tensor_copy(

@@ -19,8 +19,9 @@ ALU = mybir.AluOpType
 P = 128
 PACK = 4
 W = 512
-B_RING = 15
 JB = 128
+MEDIA_CUTS = [0, 256, 512, 1024]
+B_RING = 10
 
 
 def tile_list_vaccine_uptake_step_kernel(
@@ -35,49 +36,42 @@ def tile_list_vaccine_uptake_step_kernel(
         def held(shape, dtype, name, tag=""):
             return keep.tile(shape, dtype, name=name, tag=tag or name, align_bytes=64)
 
-        offsets = keep.tile([P, S // 16], U16, name="offsets")
-        nc.sync.dma_start(offsets[:], offs)
-
-        tab_plane = held([P, T], U8, "tab_plane")
-        nc.sync.dma_start(tab_plane[0:32, :].bitcast(I32), tab_scales.rearrange("a q t -> (a q) t").bitcast(I32))
-        nc.gpsimd.memset(tab_plane[32:64, :].bitcast(I32), 0)
-        nc.gpsimd.memset(tab_plane[64:P, :].bitcast(I32), 0)
-        wm_plane_raw = held([P, H], U8, "wm_plane_raw")
-        nc.gpsimd.memset(wm_plane_raw[:].bitcast(I32), 0)
+        table, w1_raw, media_raw, w3_raw, page = {}, {}, {}, {}, {}
+        picked, w1_q, media_q, w3_q, h_q, h_bf, state, b_sb = {}, {}, {}, {}, {}, {}, {}, {}
 
         def load_table(a):
-            tile = held([P, T], I32, f"table{a}")
-            nc.sync.dma_start(tile[:], tab_words[a].rearrange("p t i -> p (t i)").bitcast(I32))
-            return tile
+            table[a] = held([P, T], I32, f"table{a}")
+            nc.sync.dma_start(table[a][:], tab_words[a].rearrange("p t i -> p (t i)").bitcast(I32))
 
         def load_rows(src, name):
-            raw = held([P, PACK, W], F32, name)
+            raw = held([P, PACK, src.shape[1]], F32, name)
             nc.sync.dma_start(raw[:], src.rearrange("(p j) c -> p j c", j=PACK))
             return raw
 
         def load_w1(a, g):
-            return load_rows(w1[W * a : W * (a + 1), W * g : W * (g + 1)], f"w1_raw{a}{g}")
+            w1_raw[a, g] = load_rows(w1[W * a : W * (a + 1), W * g : W * (g + 1)], f"w1_raw{a}{g}")
+
+        def load_media(m):
+            media_raw[m] = load_rows(media[:, MEDIA_CUTS[m] : MEDIA_CUTS[m + 1]], f"media_raw{m}")
 
         def load_w3(g):
-            raw = held([P, PACK, W], F32, f"w3_raw{g}")
+            w3_raw[g] = held([P, PACK, W], F32, f"w3_raw{g}")
             rows = w3[W * g : W * (g + 1), :].rearrange("(b t i) n -> t b i n", t=PACK, i=4)
             for t in range(PACK):
-                nc.sync.dma_start(raw[:, t, :], rows[t])
-            return raw
+                nc.sync.dma_start(w3_raw[g][:, t, :], rows[t])
 
         def load_page(t):
-            page = held([P, T], F32, f"page{t}")
-            nc.sync.dma_start(page[:], gT.rearrange("(p t) c -> t p c", t=PACK)[t])
-            return page
+            page[t] = held([P, T], F32, f"page{t}")
+            nc.sync.dma_start(page[t][:], gT.rearrange("(p t) c -> t p c", t=PACK)[t])
 
-        table, w1_raw, media_raw, w3_raw, page = {}, {}, {}, {}, {}
-        table[0] = load_table(0)
-        media_raw[0] = load_rows(media[:, 0:W], "media_raw0")
-        wm_raw = held([P, H // 2], I32, "wm_raw")
-        nc.sync.dma_start(wm_raw[:], wm4_words[0].bitcast(I32))
-        wm_rows = wm4_scales[0].rearrange("(q r) c -> r q c", r=4)
-        for r in range(4):
-            nc.sync.dma_start(wm_plane_raw[r:P:32, :].bitcast(I32), wm_rows[r].bitcast(I32))
+        offsets = keep.tile([P, S // 16], U16, name="offsets")
+        nc.sync.dma_start(offsets[:], offs)
+        tab_plane = held([P, T], U8, "tab_plane")
+        nc.sync.dma_start(tab_plane[0:32, :].bitcast(I32), tab_scales.rearrange("a q t -> (a q) t").bitcast(I32))
+        wm_plane_raw = held([P, H], U8, "wm_plane_raw")
+        nc.gpsimd.memset(tab_plane[32:64, :].bitcast(I32), 0)
+        nc.gpsimd.memset(tab_plane[64:P, :].bitcast(I32), 0)
+        nc.gpsimd.memset(wm_plane_raw[:].bitcast(I32), 0)
         picked_rows = held([P, S], U8, "picked_rows")
         nc.vector.tensor_copy(picked_rows[:], tab_plane[:].indirect(offsets[:]))
         picked_plane = held([P, S], U8, "picked_plane")
@@ -89,34 +83,46 @@ def tile_list_vaccine_uptake_step_kernel(
                 picked_rows[16 * a + 4 * q : 16 * a + 4 * q + 4, :].bitcast(I32),
             )
 
-        page[0] = load_page(0)
-        move_rows(0, 0)
-        move_rows(0, 1)
-        w1_raw[0, 0] = load_w1(0, 0)
-        move_rows(0, 2)
-        move_rows(0, 3)
-        w1_raw[1, 0] = load_w1(1, 0)
+        wm_rows = wm4_scales[0].rearrange("(q r) c -> r q c", r=4)
+
+        def load_wm_rows(r):
+            nc.sync.dma_start(wm_plane_raw[r:P:32, :].bitcast(I32), wm_rows[r].bitcast(I32))
+
+        load_table(0)
+        wm_raw = held([P, H // 2], I32, "wm_raw")
+        nc.sync.dma_start(wm_raw[:], wm4_words[0].bitcast(I32))
+        load_media(0)
+        load_wm_rows(0)
+        load_wm_rows(1)
+        load_w1(0, 0)
+        load_wm_rows(2)
+        load_wm_rows(3)
+        load_w1(1, 0)
+        for q in range(4):
+            move_rows(0, q)
+        load_table(1)
         move_rows(1, 0)
         move_rows(1, 1)
-        table[1] = load_table(1)
+        load_media(1)
+        load_page(0)
         move_rows(1, 2)
         move_rows(1, 3)
-        media_raw[1] = load_rows(media[:, W : 2 * W], "media_raw1")
-        w1_raw[0, 1] = load_w1(0, 1)
-        page[1] = load_page(1)
-        w1_raw[1, 1] = load_w1(1, 1)
-        w3_raw[0] = load_w3(0)
-        w3_raw[1] = load_w3(1)
+        load_media(2)
+        load_w1(0, 1)
+        load_page(1)
+        load_w1(1, 1)
+        load_page(2)
+        load_w3(0)
+        load_w3(1)
         goal_sb = held([P, PACK], F32, "goal_sb")
         nc.sync.dma_start(goal_sb[:], goal.rearrange("(p t) -> p t", t=PACK))
-        page[2] = load_page(2)
-        page[3] = load_page(3)
+        load_page(3)
 
         warm = held([P, 8], F32, "warm")
         nc.gpsimd.memset(warm[:], 0.0)
         nc.scalar.activation(warm[:], warm[:], ACT.Sigmoid)
         neg_goal = held([P, PACK], F32, "neg_goal")
-        nc.scalar.mul(neg_goal[:], goal_sb[:], -1.0)
+        nc.gpsimd.tensor_scalar(neg_goal[:], goal_sb[:], -1.0, 0.0, ALU.mult, ALU.add)
 
         def copy_on(engine, out, in_):
             if engine == "vector":
@@ -125,96 +131,89 @@ def tile_list_vaccine_uptake_step_kernel(
                 nc.scalar.copy(out, in_)
 
         def quantize(grouped, name, tag=""):
-            codes = held([P, W], U32, name + "_codes", tag=tag)
-            plane = held([P, W], U8, name + "_plane")
+            width = grouped.shape[1] // PACK
+            codes = held([P, width], U32, name + "_codes", tag=tag)
+            plane = held([P, width], U8, name + "_plane")
             nc.vector.quantize_mx(out=codes[:].bitcast(FP8X4), scales=plane[:], in_=grouped[:])
             return codes, plane
 
-        def stage_tile(name):
-            return ring.tile([P, PACK * W], BF16, name=name, tag="stage", bufs=3, align_bytes=64)
-
-        def cast_w1(a, g, engine, grouped):
-            copy_on(
-                engine,
-                grouped.rearrange("p (t b i j) -> p b t j i", t=4, i=4, j=4),
-                w1_raw[a, g][:].rearrange("p j (b t i) -> p b t j i", t=4, i=4),
-            )
+        def stage_tile(name, width, own):
+            if own:
+                return held([P, width], BF16, name)
+            return ring.tile([P, width], BF16, name=name, tag="stage", bufs=3, align_bytes=64)
 
         def prep_w1(a, g, engine):
-            grouped = held([P, PACK * W], BF16, "w1_bf11") if (a, g) == (1, 1) else stage_tile(f"w1_bf{a}{g}")
-            cast_w1(a, g, engine, grouped[:])
-            return quantize(grouped, f"w1_{a}{g}")
+            grouped = stage_tile(f"w1_bf{a}{g}", PACK * W, (a, g) == (1, 1))
+            copy_on(
+                engine,
+                grouped[:].rearrange("p (t b i j) -> p b t j i", t=4, i=4, j=4),
+                w1_raw[a, g][:].rearrange("p j (b t i) -> p b t j i", t=4, i=4),
+            )
+            w1_q[a, g] = quantize(grouped, f"w1_{a}{g}")
 
-        def prep_media(half, engine):
-            grouped = held([P, PACK * W], BF16, "media_bf1") if half == 1 else stage_tile("media_bf0")
+        def prep_media(m, engine):
+            grouped = stage_tile(f"media_bf{m}", PACK * (MEDIA_CUTS[m + 1] - MEDIA_CUTS[m]), m == 2)
             copy_on(
                 engine,
                 grouped[:].rearrange("p (c i j) -> p c j i", i=4, j=4),
-                media_raw[half][:].rearrange("p j (c i) -> p c j i", i=4),
+                media_raw[m][:].rearrange("p j (c i) -> p c j i", i=4),
             )
-            return quantize(grouped, f"media_{half}")
+            media_q[m] = quantize(grouped, f"media_{m}")
 
         def prep_w3(g, engine):
-            grouped = held([P, PACK * W], BF16, "w3_bf1") if g == 1 else stage_tile("w3_bf0")
+            grouped = stage_tile(f"w3_bf{g}", PACK * W, g == 1)
             copy_on(
                 engine,
                 grouped[:].rearrange("p (t m j) -> p m j t", t=4, j=4),
                 w3_raw[g][:].rearrange("p j (m t) -> p m j t", t=4),
             )
-            return quantize(grouped, f"w3_{g}")
+            w3_q[g] = quantize(grouped, f"w3_{g}")
 
-        def gather_words(a, parts):
-            picked = held([P, S], U32, f"picked{a}")
-            for part in range(parts):
-                lo, hi = S * part // parts, S * (part + 1) // parts
-                nc.vector.tensor_copy(picked[:, lo:hi], table[a][:].bitcast(U32).indirect(offsets[:, lo // 16 : hi // 16]))
-            return picked
+        def gather_words(a, cuts):
+            picked[a] = held([P, S], U32, f"picked{a}")
+            for lo, hi in zip(cuts, cuts[1:]):
+                nc.vector.tensor_copy(picked[a][:, lo:hi], table[a][:].bitcast(U32).indirect(offsets[:, lo // 16 : hi // 16]))
+
+        state_tag = ["state0", "w1_raw00", "w1_raw10", "state3"]
 
         def gather_state(t):
             state[t] = held([P, S], F32, f"state{t}", tag=state_tag[t])
             nc.vector.tensor_copy(state[t][:], page[t][:].indirect(offsets[:]))
 
-        def make_factor(t):
-            nc.scalar.activation(
-                factor[t],
-                state[t][:],
-                ACT.Identity,
-                bias=goal_sb[:, t : t + 1],
-                scale=neg_goal[:, t : t + 1],
-            )
+        b_slot = {(1, 1): "media_raw2", (1, 2): "w1_raw11"}
 
-        state_tag = ["state0", "state1", "h_bf11", "w1_raw00"]
-        h_tag = {(0, 0): "media_bf1", (0, 1): "w1_bf11", (1, 0): "", (1, 1): "w3_bf1"}
-        h_bf = {}
-        picked, w1_q, media_q, w3_q, h_q, state = {}, {}, {}, {}, {}, {}
-
-        b_sb = {}
-
-        def make_b(g, half):
-            for jb in range(W // JB):
-                local = slice(JB * jb, JB * (jb + 1))
-                b_bank = psum.tile([P, PACK, JB], F32, name=f"b_bank{g}{half}{jb}", tag="b_bank", bufs=2)
+        def make_b(g, m):
+            first = MEDIA_CUTS[m] // JB
+            late = held([P, W // JB, JB, PACK], F32, f"b_late{m}", tag=b_slot[g, m]) if (g, m) in b_slot else None
+            for jb in range(MEDIA_CUTS[m] // JB, MEDIA_CUTS[m + 1] // JB):
+                local = slice(JB * jb - MEDIA_CUTS[m], JB * (jb + 1) - MEDIA_CUTS[m])
+                b_bank = psum.tile([P, PACK, JB], F32, name=f"b_bank{g}{jb}", tag="b_bank", bufs=3)
                 for t in range(PACK):
                     r0 = W * g + P * t
                     nc.tensor.matmul_mx(
                         out=b_bank[:, t, :],
                         lhsT=wm_codes[:].bitcast(U8)[:, 2 * r0 : 2 * (r0 + P)].bitcast(FP4X4),
                         lhsT_scale=wm_plane[:, r0 : r0 + P],
-                        rhs=media_q[half][0][:, local].bitcast(FP8X4),
-                        rhs_scale=media_q[half][1][:, local],
+                        rhs=media_q[m][0][:, local].bitcast(FP8X4),
+                        rhs_scale=media_q[m][1][:, local],
                         start=True,
                         stop=True,
                     )
-                slot = ring.tile([P, JB, PACK], F32, name=f"b_sb{g}{half}{jb}", tag="b_sb", bufs=B_RING)
-                b_sb[g, half, jb] = slot[:]
-                nc.scalar.copy(b_sb[g, half, jb], b_bank[:].rearrange("p t n -> p n t"))
+                if late is None:
+                    b_sb[g, jb] = ring.tile([P, JB, PACK], F32, name=f"b_sb{g}{jb}", tag="b_sb", bufs=B_RING)[:]
+                else:
+                    b_sb[g, jb] = late[:, jb - first]
+                nc.scalar.copy(b_sb[g, jb], b_bank[:].rearrange("p t n -> p n t"))
 
-        def make_h(g, half):
-            grouped = held([P, PACK * W], BF16, f"h_bf{g}{half}", tag=f"table{half}" if g == 0 else "")
-            h_bf[g, half] = grouped
-            for jb in range(W // JB):
-                cols = slice(W * half + JB * jb, W * half + JB * (jb + 1))
-                a_bank = psum.tile([P, PACK, JB], F32, name=f"a_bank{g}{half}{jb}", tag="a_bank", bufs=6)
+        h_slot = {(0, 0): "table0", (0, 1): "table1", (1, 0): "media_raw0", (1, 1): "media_raw1"}
+
+        def make_h(g, blocks):
+            for jb in blocks:
+                half, local = divmod(jb, W // JB)
+                if local == 0:
+                    h_bf[g, half] = held([P, PACK * W], BF16, f"h_bf{g}{half}", tag=h_slot[g, half])
+                cols = slice(JB * jb, JB * (jb + 1))
+                a_bank = psum.tile([P, PACK, JB], F32, name=f"a_bank{g}{jb}", tag="a_bank", bufs=5)
                 for a in range(2):
                     for t in range(PACK):
                         nc.tensor.matmul_mx(
@@ -227,60 +226,79 @@ def tile_list_vaccine_uptake_step_kernel(
                             stop=(a == 1 and t == PACK - 1),
                         )
                 nc.vector.tensor_tensor(
-                    grouped[:, PACK * JB * jb : PACK * JB * (jb + 1)].rearrange("p (n t) -> p n t", t=PACK),
+                    h_bf[g, half][:, PACK * JB * local : PACK * JB * (local + 1)].rearrange("p (n t) -> p n t", t=PACK),
                     a_bank[:].rearrange("p t n -> p n t"),
-                    b_sb[g, half, jb],
+                    b_sb[g, jb],
                     ALU.max,
                 )
+
+        h_tag = {(0, 0): "media_bf2", (0, 1): "w1_bf11", (1, 0): "", (1, 1): "w3_bf1"}
 
         def quantize_h(g, half):
             h_q[g, half] = quantize(h_bf[g, half], f"h_{g}{half}", tag=h_tag[g, half])
 
-        picked[0] = gather_words(0, 1)
+        gather_words(0, [0, S])
         wm_codes = held([P, H // 2], I32, "wm_codes")
         nc.vector.tensor_copy(
             wm_codes[:].rearrange("p (g t b w) -> p g b t w", g=2, t=4, w=2),
             wm_raw[:].rearrange("p (g b t w) -> p g b t w", g=2, t=4, w=2),
         )
+        prep_media(0, "scalar")
         wm_plane = held([P, H], U8, "wm_plane")
         nc.vector.tensor_copy(
             wm_plane[:].bitcast(I32).rearrange("p (g t b) -> p g b t", g=2, t=4),
             wm_plane_raw[:].bitcast(I32).rearrange("p (g b t) -> p g b t", g=2, t=4),
         )
-        media_q[0] = prep_media(0, "scalar")
-        gather_state(0)
+        prep_w1(0, 0, "vector")
         make_b(0, 0)
-        w1_q[0, 0] = prep_w1(0, 0, "vector")
-        w1_q[1, 0] = prep_w1(1, 0, "vector")
-        picked[1] = gather_words(1, 2)
+        prep_w1(1, 0, "vector")
         make_b(1, 0)
-
-        make_h(0, 0)
-        media_q[1] = prep_media(1, "scalar")
-        quantize_h(0, 0)
-        w1_q[0, 1] = prep_w1(0, 1, "scalar")
-        gather_state(1)
+        gather_words(1, [0, 256, S])
+        prep_media(1, "scalar")
+        make_h(0, [0, 1])
         make_b(0, 1)
-        make_h(0, 1)
-        w1_q[1, 1] = prep_w1(1, 1, "scalar")
-        quantize_h(0, 1)
-        w3_q[0] = prep_w3(0, "scalar")
+        gather_state(0)
+        make_h(0, [2, 3])
+        prep_media(2, "scalar")
         make_b(1, 1)
-        make_h(1, 0)
-        make_h(1, 1)
-        w3_q[1] = prep_w3(1, "scalar")
+        quantize_h(0, 0)
+        gather_state(1)
+        prep_w1(0, 1, "scalar")
+        make_b(0, 2)
+        make_h(0, [4, 5, 6, 7])
+        prep_w1(1, 1, "scalar")
+        quantize_h(0, 1)
+        gather_state(2)
+        make_b(1, 2)
+        make_h(1, range(S // JB))
+        prep_w3(0, "scalar")
+        prep_w3(1, "scalar")
         quantize_h(1, 0)
         quantize_h(1, 1)
+        gather_state(3)
 
+        blend_pair = [held([P, 2, S], F32, f"blend_pair{u}", tag=f"w1_raw{u}1") for u in range(2)]
+        blend = [blend_pair[t // 2][:, t % 2, :] for t in range(PACK)]
+        early = held([P, PACK - 1, S], F32, "factor_early", tag="table1")
+        factor = [early[:, t, :] for t in range(PACK - 1)]
+        factor.append(held([P, S], F32, "factor_last", tag="picked1")[:])
 
-        reuse = ["w1_raw00", "w1_raw10", "w1_raw01", "w1_raw11"]
-        blend = [held([P, S], F32, f"blend{t}", tag=reuse[t]) for t in range(PACK)]
-        factor_pair = [held([P, 2, S], F32, f"factor_pair{u}", tag=f"w3_raw{1 - u}") for u in range(2)]
-        factor = [factor_pair[t // 2][:, t % 2, :] for t in range(PACK)]
-        make_factor(0)
+        def make_factor(t):
+            if t < PACK - 1:
+                nc.gpsimd.tensor_scalar(
+                    factor[t], state[t][:], neg_goal[:, t : t + 1], goal_sb[:, t : t + 1], ALU.mult, ALU.add
+                )
+            else:
+                nc.scalar.activation(
+                    factor[t], state[t][:], ACT.Identity, bias=goal_sb[:, t : t + 1], scale=neg_goal[:, t : t + 1]
+                )
+
+        for t in range(PACK - 1):
+            make_factor(t)
         for t in range(PACK):
             for half in range(2):
-                e_bank = psum.tile([P, W], F32, name=f"e_bank{t}{half}", tag="a_bank", bufs=6)
+                tag, bufs = ("a_bank", 5) if 2 * t + half < 5 else ("b_bank", 3)
+                e_bank = psum.tile([P, W], F32, name=f"e_bank{t}{half}", tag=tag, bufs=bufs)
                 for g in range(2):
                     nc.tensor.matmul_mx(
                         out=e_bank[:],
@@ -292,15 +310,13 @@ def tile_list_vaccine_uptake_step_kernel(
                         stop=(g == 1),
                     )
                 nc.scalar.activation(blend[t][:, W * half : W * (half + 1)], e_bank[:], ACT.Sigmoid)
-        make_factor(1)
-        gather_state(2)
-        make_factor(2)
+        make_factor(PACK - 1)
 
         half_t = T // 2
         y_bf = [held([P, half_t, PACK], BF16, f"y_bf{c}", tag=["w3_bf1", "w3_1_codes"][c]) for c in range(2)]
         y_rows = out_0.rearrange("(p t) c -> t p c", t=PACK)
         for t in range(PACK):
-            nc.vector.tensor_tensor(page[t][:].indirect(offsets[:]), blend[t][:], factor[t], ALU.mult)
+            nc.vector.tensor_tensor(page[t][:].indirect(offsets[:]), blend[t], factor[t], ALU.mult)
             nc.sync.dma_start(y_rows[t], page[t][:])
             if t < PACK - 1:
                 for c in range(2):
@@ -309,12 +325,9 @@ def tile_list_vaccine_uptake_step_kernel(
                         nc.scalar.copy(y_bf[c][:, :, t : t + 2], piece.unsqueeze(2).to_broadcast([P, half_t, 2]))
                     else:
                         nc.scalar.copy(y_bf[c][:, :, t], piece)
-            if t == 1:
-                gather_state(PACK - 1)
-                make_factor(PACK - 1)
         last = PACK - 1
         y_plane = held([P, T], U8, "y_plane")
-        y_codes = held([P, T], I32, "y_codes", tag="media_raw0")
+        y_codes = held([P, T], I32, "y_codes", tag="media_raw2")
         y_words = out_1[0].rearrange("p m t -> p (m t)").bitcast(I32)
         for x in range(0, half_t, W):
             nc.vector.tensor_copy(y_bf[0][:, x : x + W, last], page[last][:, x : x + W])

@@ -91,38 +91,40 @@ def tile_list_vaccine_uptake_step_kernel(
         load_table(0)
         wm_raw = held([P, H // 2], I32, "wm_raw")
         nc.sync.dma_start(wm_raw[:], wm4_words[0].bitcast(I32))
-        load_media(0)
         load_wm_rows(0)
         load_wm_rows(1)
-        load_w1(0, 0)
+        load_media(0)
         load_wm_rows(2)
         load_wm_rows(3)
+        load_w1(0, 0)
+        move_rows(0, 0)
+        move_rows(0, 1)
         load_w1(1, 0)
-        for q in range(4):
-            move_rows(0, q)
-        load_table(1)
+        move_rows(0, 2)
+        move_rows(0, 3)
         move_rows(1, 0)
+        load_table(1)
         move_rows(1, 1)
-        load_media(1)
-        load_page(0)
         move_rows(1, 2)
         move_rows(1, 3)
+        load_media(1)
+        load_page(0)
         load_media(2)
         load_w1(0, 1)
         load_page(1)
         load_w1(1, 1)
-        load_page(2)
         load_w3(0)
         load_w3(1)
         goal_sb = held([P, PACK], F32, "goal_sb")
         nc.sync.dma_start(goal_sb[:], goal.rearrange("(p t) -> p t", t=PACK))
+        load_page(2)
         load_page(3)
 
         warm = held([P, 8], F32, "warm")
         nc.gpsimd.memset(warm[:], 0.0)
         nc.scalar.activation(warm[:], warm[:], ACT.Sigmoid)
         neg_goal = held([P, PACK], F32, "neg_goal")
-        nc.gpsimd.tensor_scalar(neg_goal[:], goal_sb[:], -1.0, 0.0, ALU.mult, ALU.add)
+        nc.scalar.mul(neg_goal[:], goal_sb[:], -1.0)
 
         def copy_on(engine, out, in_):
             if engine == "vector":
@@ -174,7 +176,7 @@ def tile_list_vaccine_uptake_step_kernel(
             for lo, hi in zip(cuts, cuts[1:]):
                 nc.vector.tensor_copy(picked[a][:, lo:hi], table[a][:].bitcast(U32).indirect(offsets[:, lo // 16 : hi // 16]))
 
-        state_tag = ["state0", "w1_raw00", "w1_raw10", "state3"]
+        state_tag = ["state0", "state1", "media_raw1", "w1_raw00"]
 
         def gather_state(t):
             state[t] = held([P, S], F32, f"state{t}", tag=state_tag[t])
@@ -187,7 +189,7 @@ def tile_list_vaccine_uptake_step_kernel(
             late = held([P, W // JB, JB, PACK], F32, f"b_late{m}", tag=b_slot[g, m]) if (g, m) in b_slot else None
             for jb in range(MEDIA_CUTS[m] // JB, MEDIA_CUTS[m + 1] // JB):
                 local = slice(JB * jb - MEDIA_CUTS[m], JB * (jb + 1) - MEDIA_CUTS[m])
-                b_bank = psum.tile([P, PACK, JB], F32, name=f"b_bank{g}{jb}", tag="b_bank", bufs=3)
+                b_bank = psum.tile([P, PACK, JB], F32, name=f"b_bank{g}{jb}", tag="b_bank", bufs=2)
                 for t in range(PACK):
                     r0 = W * g + P * t
                     nc.tensor.matmul_mx(
@@ -213,7 +215,7 @@ def tile_list_vaccine_uptake_step_kernel(
                 if local == 0:
                     h_bf[g, half] = held([P, PACK * W], BF16, f"h_bf{g}{half}", tag=h_slot[g, half])
                 cols = slice(JB * jb, JB * (jb + 1))
-                a_bank = psum.tile([P, PACK, JB], F32, name=f"a_bank{g}{jb}", tag="a_bank", bufs=5)
+                a_bank = psum.tile([P, PACK, JB], F32, name=f"a_bank{g}{jb}", tag="a_bank", bufs=6)
                 for a in range(2):
                     for t in range(PACK):
                         nc.tensor.matmul_mx(
@@ -262,43 +264,33 @@ def tile_list_vaccine_uptake_step_kernel(
         prep_media(2, "scalar")
         make_b(1, 1)
         quantize_h(0, 0)
-        gather_state(1)
-        prep_w1(0, 1, "scalar")
+        prep_w1(0, 1, "vector")
         make_b(0, 2)
         make_h(0, [4, 5, 6, 7])
+        gather_state(1)
         prep_w1(1, 1, "scalar")
         quantize_h(0, 1)
-        gather_state(2)
         make_b(1, 2)
         make_h(1, range(S // JB))
         prep_w3(0, "scalar")
         prep_w3(1, "scalar")
         quantize_h(1, 0)
         quantize_h(1, 1)
-        gather_state(3)
 
-        blend_pair = [held([P, 2, S], F32, f"blend_pair{u}", tag=f"w1_raw{u}1") for u in range(2)]
-        blend = [blend_pair[t // 2][:, t % 2, :] for t in range(PACK)]
-        early = held([P, PACK - 1, S], F32, "factor_early", tag="table1")
-        factor = [early[:, t, :] for t in range(PACK - 1)]
-        factor.append(held([P, S], F32, "factor_last", tag="picked1")[:])
+        reuse = ["w1_raw00", "w1_raw10", "w1_raw01", "w1_raw11"]
+        blend = [held([P, S], F32, f"blend{t}", tag=reuse[t])[:] for t in range(PACK)]
+        factor_pair = [held([P, 2, S], F32, f"factor_pair{u}", tag=f"w3_raw{1 - u}") for u in range(2)]
+        factor = [factor_pair[t // 2][:, t % 2, :] for t in range(PACK)]
 
         def make_factor(t):
-            if t < PACK - 1:
-                nc.gpsimd.tensor_scalar(
-                    factor[t], state[t][:], neg_goal[:, t : t + 1], goal_sb[:, t : t + 1], ALU.mult, ALU.add
-                )
-            else:
-                nc.scalar.activation(
-                    factor[t], state[t][:], ACT.Identity, bias=goal_sb[:, t : t + 1], scale=neg_goal[:, t : t + 1]
-                )
+            nc.scalar.activation(
+                factor[t], state[t][:], ACT.Identity, bias=goal_sb[:, t : t + 1], scale=neg_goal[:, t : t + 1]
+            )
 
-        for t in range(PACK - 1):
-            make_factor(t)
+        make_factor(0)
         for t in range(PACK):
             for half in range(2):
-                tag, bufs = ("a_bank", 5) if 2 * t + half < 5 else ("b_bank", 3)
-                e_bank = psum.tile([P, W], F32, name=f"e_bank{t}{half}", tag=tag, bufs=bufs)
+                e_bank = psum.tile([P, W], F32, name=f"e_bank{t}{half}", tag="a_bank", bufs=6)
                 for g in range(2):
                     nc.tensor.matmul_mx(
                         out=e_bank[:],
@@ -310,7 +302,9 @@ def tile_list_vaccine_uptake_step_kernel(
                         stop=(g == 1),
                     )
                 nc.scalar.activation(blend[t][:, W * half : W * (half + 1)], e_bank[:], ACT.Sigmoid)
-        make_factor(PACK - 1)
+        make_factor(1)
+        gather_state(2)
+        make_factor(2)
 
         half_t = T // 2
         y_bf = [held([P, half_t, PACK], BF16, f"y_bf{c}", tag=["w3_bf1", "w3_1_codes"][c]) for c in range(2)]
@@ -325,6 +319,9 @@ def tile_list_vaccine_uptake_step_kernel(
                         nc.scalar.copy(y_bf[c][:, :, t : t + 2], piece.unsqueeze(2).to_broadcast([P, half_t, 2]))
                     else:
                         nc.scalar.copy(y_bf[c][:, :, t], piece)
+            if t == 1:
+                gather_state(PACK - 1)
+                make_factor(PACK - 1)
         last = PACK - 1
         y_plane = held([P, T], U8, "y_plane")
         y_codes = held([P, T], I32, "y_codes", tag="media_raw2")

@@ -142,10 +142,13 @@ def tile_list_vaccine_uptake_step_kernel(
         def stage_tile(name, width, own):
             if own:
                 return held([P, width], BF16, name)
-            return ring.tile([P, width], BF16, name=name, tag="stage", bufs=3, align_bytes=64)
+            return ring.tile([P, width], BF16, name=name, tag="stage", bufs=2, align_bytes=64)
 
         def prep_w1(a, g, engine):
-            grouped = stage_tile(f"w1_bf{a}{g}", PACK * W, (a, g) == (1, 1))
+            if (a, g) == (0, 1):
+                grouped = held([P, PACK * W], BF16, "w1_bf01", tag="media_bf2")
+            else:
+                grouped = stage_tile(f"w1_bf{a}{g}", PACK * W, (a, g) == (1, 1))
             copy_on(
                 engine,
                 grouped[:].rearrange("p (t b i j) -> p b t j i", t=4, i=4, j=4),
@@ -154,7 +157,7 @@ def tile_list_vaccine_uptake_step_kernel(
             w1_q[a, g] = quantize(grouped, f"w1_{a}{g}")
 
         def prep_media(m, engine):
-            grouped = stage_tile(f"media_bf{m}", PACK * (MEDIA_CUTS[m + 1] - MEDIA_CUTS[m]), m == 2)
+            grouped = stage_tile(f"media_bf{m}", PACK * (MEDIA_CUTS[m + 1] - MEDIA_CUTS[m]), m >= 1)
             copy_on(
                 engine,
                 grouped[:].rearrange("p (c i j) -> p c j i", i=4, j=4),
@@ -201,13 +204,13 @@ def tile_list_vaccine_uptake_step_kernel(
                         start=True,
                         stop=True,
                     )
-                if late is None:
+                if late is None or (m == 2 and jb - first < 1):
                     b_sb[g, jb] = ring.tile([P, JB, PACK], F32, name=f"b_sb{g}{jb}", tag="b_sb", bufs=B_RING)[:]
                 else:
                     b_sb[g, jb] = late[:, jb - first]
                 nc.scalar.copy(b_sb[g, jb], b_bank[:].rearrange("p t n -> p n t"))
 
-        h_slot = {(0, 0): "table0", (0, 1): "table1", (1, 0): "media_raw0", (1, 1): "media_raw1"}
+        h_slot = {(0, 0): "media_bf1", (0, 1): "table1", (1, 0): "media_raw0", (1, 1): "media_raw1"}
 
         def make_h(g, blocks):
             for jb in blocks:
@@ -234,7 +237,7 @@ def tile_list_vaccine_uptake_step_kernel(
                     ALU.max,
                 )
 
-        h_tag = {(0, 0): "media_bf2", (0, 1): "w1_bf11", (1, 0): "", (1, 1): "w3_bf1"}
+        h_tag = {(0, 0): "", (0, 1): "w1_bf11", (1, 0): "", (1, 1): "w3_bf1"}
 
         def quantize_h(g, half):
             h_q[g, half] = quantize(h_bf[g, half], f"h_{g}{half}", tag=h_tag[g, half])
@@ -261,18 +264,18 @@ def tile_list_vaccine_uptake_step_kernel(
         make_b(0, 1)
         gather_state(0)
         make_h(0, [2, 3])
+        quantize_h(0, 0)
         prep_media(2, "scalar")
         make_b(1, 1)
-        quantize_h(0, 0)
         prep_w1(0, 1, "vector")
         make_b(0, 2)
         make_h(0, [4, 5, 6, 7])
         gather_state(1)
         prep_w1(1, 1, "scalar")
         quantize_h(0, 1)
+        prep_w3(0, "scalar")
         make_b(1, 2)
         make_h(1, range(S // JB))
-        prep_w3(0, "scalar")
         prep_w3(1, "scalar")
         quantize_h(1, 0)
         quantize_h(1, 1)

@@ -269,8 +269,8 @@ def tile_list_vaccine_uptake_step_kernel(
         make_b(1, 1)
         prep_w1(0, 1, "vector")
         make_b(0, 2)
-        make_h(0, [4, 5, 6, 7])
         gather_state(1)
+        make_h(0, [4, 5, 6, 7])
         prep_w1(1, 1, "scalar")
         quantize_h(0, 1)
         prep_w3(0, "scalar")

@@ -192,7 +192,7 @@ def tile_list_vaccine_uptake_step_kernel(
             late = held([P, W // JB, JB, PACK], F32, f"b_late{m}", tag=b_slot[g, m]) if (g, m) in b_slot else None
             for jb in range(MEDIA_CUTS[m] // JB, MEDIA_CUTS[m + 1] // JB):
                 local = slice(JB * jb - MEDIA_CUTS[m], JB * (jb + 1) - MEDIA_CUTS[m])
-                b_bank = psum.tile([P, PACK, JB], F32, name=f"b_bank{g}{jb}", tag="b_bank", bufs=2)
+                b_bank = psum.tile([P, PACK, JB], F32, name=f"b_bank{g}{jb}", tag="b_bank", bufs=3)
                 for t in range(PACK):
                     r0 = W * g + P * t
                     nc.tensor.matmul_mx(
@@ -218,7 +218,7 @@ def tile_list_vaccine_uptake_step_kernel(
                 if local == 0:
                     h_bf[g, half] = held([P, PACK * W], BF16, f"h_bf{g}{half}", tag=h_slot[g, half])
                 cols = slice(JB * jb, JB * (jb + 1))
-                a_bank = psum.tile([P, PACK, JB], F32, name=f"a_bank{g}{jb}", tag="a_bank", bufs=6)
+                a_bank = psum.tile([P, PACK, JB], F32, name=f"a_bank{g}{jb}", tag="a_bank", bufs=5)
                 for a in range(2):
                     for t in range(PACK):
                         nc.tensor.matmul_mx(
@@ -293,7 +293,8 @@ def tile_list_vaccine_uptake_step_kernel(
         make_factor(0)
         for t in range(PACK):
             for half in range(2):
-                e_bank = psum.tile([P, W], F32, name=f"e_bank{t}{half}", tag="a_bank", bufs=6)
+                tag, bufs = ("a_bank", 5) if 2 * t + half < 5 else ("b_bank", 3)
+                e_bank = psum.tile([P, W], F32, name=f"e_bank{t}{half}", tag=tag, bufs=bufs)
                 for g in range(2):
                     nc.tensor.matmul_mx(
                         out=e_bank[:],

@@ -77,10 +77,10 @@ def tile_list_vaccine_uptake_step_kernel(
         picked_plane = held([P, S], U8, "picked_plane")
         nc.gpsimd.memset(picked_plane[:].bitcast(I32), 0)
 
-        def move_rows(a, q):
+        def move_rows(a, r):
             nc.sync.dma_start(
-                picked_plane[32 * q + 4 * a : 32 * q + 4 * a + 4, :].bitcast(I32),
-                picked_rows[16 * a + 4 * q : 16 * a + 4 * q + 4, :].bitcast(I32),
+                picked_plane[4 * a + r : P : 32, :].bitcast(I32),
+                picked_rows[16 * a + r : 16 * a + 16 : 4, :].bitcast(I32),
             )
 
         wm_rows = wm4_scales[0].rearrange("(q r) c -> r q c", r=4)

@@ -99,8 +99,8 @@ def tile_list_vaccine_uptake_step_kernel(
         load_w1(0, 0)
         move_rows(0, 0)
         move_rows(0, 1)
-        load_w1(1, 0)
         move_rows(0, 2)
+        load_w1(1, 0)
         move_rows(0, 3)
         move_rows(1, 0)
         load_table(1)

@@ -20,8 +20,8 @@ P = 128
 PACK = 4
 W = 512
 JB = 128
-MEDIA_CUTS = [0, 256, 512, 1024]
-B_RING = 10
+MEDIA_CUTS = [0, 256, 512, 768, 1024]
+B_RING = 9
 
 
 def tile_list_vaccine_uptake_step_kernel(
@@ -74,12 +74,13 @@ def tile_list_vaccine_uptake_step_kernel(
         nc.gpsimd.memset(wm_plane_raw[:].bitcast(I32), 0)
         picked_rows = held([P, S], U8, "picked_rows")
         nc.vector.tensor_copy(picked_rows[:], tab_plane[:].indirect(offsets[:]))
-        picked_plane = held([P, S], U8, "picked_plane")
-        nc.gpsimd.memset(picked_plane[:].bitcast(I32), 0)
+        picked_plane = [held([P, S], U8, f"picked_plane{a}") for a in range(2)]
+        for plane in picked_plane:
+            nc.gpsimd.memset(plane[:].bitcast(I32), 0)
 
         def move_rows(a, r):
             nc.sync.dma_start(
-                picked_plane[4 * a + r : P : 32, :].bitcast(I32),
+                picked_plane[a][4 * a + r : P : 32, :].bitcast(I32),
                 picked_rows[16 * a + r : 16 * a + 16 : 4, :].bitcast(I32),
             )
 
@@ -111,6 +112,7 @@ def tile_list_vaccine_uptake_step_kernel(
         load_page(0)
         load_media(2)
         load_w1(0, 1)
+        load_media(3)
         load_page(1)
         load_w1(1, 1)
         load_w3(0)
@@ -145,10 +147,7 @@ def tile_list_vaccine_uptake_step_kernel(
             return ring.tile([P, width], BF16, name=name, tag="stage", bufs=2, align_bytes=64)
 
         def prep_w1(a, g, engine):
-            if (a, g) == (0, 1):
-                grouped = held([P, PACK * W], BF16, "w1_bf01", tag="media_bf2")
-            else:
-                grouped = stage_tile(f"w1_bf{a}{g}", PACK * W, (a, g) == (1, 1))
+            grouped = stage_tile(f"w1_bf{a}{g}", PACK * W, (a, g) == (1, 1))
             copy_on(
                 engine,
                 grouped[:].rearrange("p (t b i j) -> p b t j i", t=4, i=4, j=4),
@@ -185,14 +184,19 @@ def tile_list_vaccine_uptake_step_kernel(
             state[t] = held([P, S], F32, f"state{t}", tag=state_tag[t])
             nc.vector.tensor_copy(state[t][:], page[t][:].indirect(offsets[:]))
 
-        b_slot = {(1, 1): "media_raw2", (1, 2): "w1_raw11"}
+        b_late = {2: (2, "media_raw2"), 5: (3, "w1_raw11")}
+        late = {}
+
+        a_banks = [[0, 1, 6, 7, 2, 3, 6, 7], [2, 3, 6, 7, 1, 5, 4, 0]]
+        b_banks = [[2, 3, 6, 7, 0, 1, 0, 1], [4, 5, 2, 3, 4, 5, 4, 0]]
+
+        def bank(shape, name, number):
+            return psum.tile(shape, F32, name=name, offset=4 * W * number)
 
         def make_b(g, m):
-            first = MEDIA_CUTS[m] // JB
-            late = held([P, W // JB, JB, PACK], F32, f"b_late{m}", tag=b_slot[g, m]) if (g, m) in b_slot else None
             for jb in range(MEDIA_CUTS[m] // JB, MEDIA_CUTS[m + 1] // JB):
                 local = slice(JB * jb - MEDIA_CUTS[m], JB * (jb + 1) - MEDIA_CUTS[m])
-                b_bank = psum.tile([P, PACK, JB], F32, name=f"b_bank{g}{jb}", tag="b_bank", bufs=3)
+                b_bank = bank([P, PACK, JB], f"b_bank{g}{jb}", b_banks[g][jb])
                 for t in range(PACK):
                     r0 = W * g + P * t
                     nc.tensor.matmul_mx(
@@ -204,21 +208,28 @@ def tile_list_vaccine_uptake_step_kernel(
                         start=True,
                         stop=True,
                     )
-                if late is None or (m == 2 and jb - first < 1):
-                    b_sb[g, jb] = ring.tile([P, JB, PACK], F32, name=f"b_sb{g}{jb}", tag="b_sb", bufs=B_RING)[:]
+                if g == 1 and jb in b_late:
+                    count, tag = b_late[jb]
+                    shared = held([P, count, JB, PACK], F32, f"b_late{jb}", tag=tag)
+                    late.update({jb + n: shared[:, n] for n in range(count)})
+                if g == 1 and jb in late:
+                    b_sb[g, jb] = late[jb]
                 else:
-                    b_sb[g, jb] = late[:, jb - first]
+                    b_sb[g, jb] = ring.tile([P, JB, PACK], F32, name=f"b_sb{g}{jb}", tag="b_sb", bufs=B_RING)[:]
                 nc.scalar.copy(b_sb[g, jb], b_bank[:].rearrange("p t n -> p n t"))
 
-        h_slot = {(0, 0): "media_bf1", (0, 1): "table1", (1, 0): "media_raw0", (1, 1): "media_raw1"}
+        h_tiles = {(0, 0): (2, "media_bf1"), (0, 2): (2, "media_bf2"), (0, 4): (4, "media_bf3")}
+        h_tiles.update({(1, 0): (4, "media_raw0"), (1, 4): (4, "media_raw1")})
 
         def make_h(g, blocks):
             for jb in blocks:
-                half, local = divmod(jb, W // JB)
+                first = max(f for gg, f in h_tiles if gg == g and f <= jb)
+                local = jb - first
                 if local == 0:
-                    h_bf[g, half] = held([P, PACK * W], BF16, f"h_bf{g}{half}", tag=h_slot[g, half])
+                    count, tag = h_tiles[g, first]
+                    h_bf[g, first] = held([P, PACK * JB * count], BF16, f"h_bf{g}{first}", tag=tag)
                 cols = slice(JB * jb, JB * (jb + 1))
-                a_bank = psum.tile([P, PACK, JB], F32, name=f"a_bank{g}{jb}", tag="a_bank", bufs=5)
+                a_bank = bank([P, PACK, JB], f"a_bank{g}{jb}", a_banks[g][jb])
                 for a in range(2):
                     for t in range(PACK):
                         nc.tensor.matmul_mx(
@@ -226,21 +237,27 @@ def tile_list_vaccine_uptake_step_kernel(
                             lhsT=w1_q[a, g][0][:, P * t : P * (t + 1)].bitcast(FP8X4),
                             lhsT_scale=w1_q[a, g][1][:, P * t : P * (t + 1)],
                             rhs=picked[a][:, cols].bitcast(FP8X4),
-                            rhs_scale=picked_plane[4 * a : P, cols],
+                            rhs_scale=picked_plane[a][4 * a : P, cols],
                             start=(a == 0 and t == 0),
                             stop=(a == 1 and t == PACK - 1),
                         )
                 nc.vector.tensor_tensor(
-                    h_bf[g, half][:, PACK * JB * local : PACK * JB * (local + 1)].rearrange("p (n t) -> p n t", t=PACK),
+                    h_bf[g, first][:, PACK * JB * local : PACK * JB * (local + 1)].rearrange("p (n t) -> p n t", t=PACK),
                     a_bank[:].rearrange("p t n -> p n t"),
                     b_sb[g, jb],
                     ALU.max,
                 )
 
-        h_tag = {(0, 0): "", (0, 1): "w1_bf11", (1, 0): "", (1, 1): "w3_bf1"}
+        h_tag = {(0, 0): "w1_raw01", (0, 1): "w1_bf11", (1, 0): "", (1, 1): "w3_bf1"}
 
         def quantize_h(g, half):
-            h_q[g, half] = quantize(h_bf[g, half], f"h_{g}{half}", tag=h_tag[g, half])
+            codes = held([P, W], U32, f"h_{g}{half}_codes", tag=h_tag[g, half])
+            plane = held([P, W], U8, f"h_{g}{half}_plane")
+            for (gg, first), (count, tag) in h_tiles.items():
+                if gg == g and first * JB // W == half:
+                    cols = slice(first * JB - W * half, (first + count) * JB - W * half)
+                    nc.vector.quantize_mx(out=codes[:, cols].bitcast(FP8X4), scales=plane[:, cols], in_=h_bf[g, first][:])
+            h_q[g, half] = codes, plane
 
         gather_words(0, [0, S])
         wm_codes = held([P, H // 2], I32, "wm_codes")
@@ -263,18 +280,22 @@ def tile_list_vaccine_uptake_step_kernel(
         make_h(0, [0, 1])
         make_b(0, 1)
         gather_state(0)
-        make_h(0, [2, 3])
-        quantize_h(0, 0)
         prep_media(2, "scalar")
+        make_h(0, [2, 3])
         make_b(1, 1)
-        prep_w1(0, 1, "vector")
         make_b(0, 2)
+        quantize_h(0, 0)
+        prep_w1(0, 1, "vector")
+        prep_media(3, "scalar")
+        make_h(0, [4, 5])
+        make_b(0, 3)
+        make_b(1, 2)
         gather_state(1)
-        make_h(0, [4, 5, 6, 7])
+        make_h(0, [6, 7])
         prep_w1(1, 1, "scalar")
         quantize_h(0, 1)
         prep_w3(0, "scalar")
-        make_b(1, 2)
+        make_b(1, 3)
         make_h(1, range(S // JB))
         prep_w3(1, "scalar")
         quantize_h(1, 0)
@@ -293,8 +314,7 @@ def tile_list_vaccine_uptake_step_kernel(
         make_factor(0)
         for t in range(PACK):
             for half in range(2):
-                tag, bufs = ("a_bank", 5) if 2 * t + half < 5 else ("b_bank", 3)
-                e_bank = psum.tile([P, W], F32, name=f"e_bank{t}{half}", tag=tag, bufs=bufs)
+                e_bank = bank([P, W], f"e_bank{t}{half}", a_banks[1][2 * t + half])
                 for g in range(2):
                     nc.tensor.matmul_mx(
                         out=e_bank[:],
@@ -328,7 +348,7 @@ def tile_list_vaccine_uptake_step_kernel(
                 make_factor(PACK - 1)
         last = PACK - 1
         y_plane = held([P, T], U8, "y_plane")
-        y_codes = held([P, T], I32, "y_codes", tag="media_raw2")
+        y_codes = held([P, T], I32, "y_codes", tag="table0")
         y_words = out_1[0].rearrange("p m t -> p (m t)").bitcast(I32)
         for x in range(0, half_t, W):
             nc.vector.tensor_copy(y_bf[0][:, x : x + W, last], page[last][:, x : x + W])

@@ -52,7 +52,11 @@ def tile_list_vaccine_uptake_step_kernel(
             w1_raw[a, g] = load_rows(w1[W * a : W * (a + 1), W * g : W * (g + 1)], f"w1_raw{a}{g}")
 
         def load_media(m):
-            media_raw[m] = load_rows(media[:, MEDIA_CUTS[m] : MEDIA_CUTS[m + 1]], f"media_raw{m}")
+            if m < 2:
+                media_raw[m] = load_rows(media[:, MEDIA_CUTS[m] : MEDIA_CUTS[m + 1]], f"media_raw{m}")[:]
+            else:
+                both = load_rows(media[:, W:], "media_raw2")
+                media_raw[2], media_raw[3] = both[:, :, : W // 2], both[:, :, W // 2 :]
 
         def load_w3(g):
             w3_raw[g] = held([P, PACK, W], F32, f"w3_raw{g}")
@@ -112,7 +116,6 @@ def tile_list_vaccine_uptake_step_kernel(
         load_page(0)
         load_media(2)
         load_w1(0, 1)
-        load_media(3)
         load_page(1)
         load_w1(1, 1)
         load_w3(0)
@@ -147,7 +150,10 @@ def tile_list_vaccine_uptake_step_kernel(
             return ring.tile([P, width], BF16, name=name, tag="stage", bufs=2, align_bytes=64)
 
         def prep_w1(a, g, engine):
-            grouped = stage_tile(f"w1_bf{a}{g}", PACK * W, (a, g) == (1, 1))
+            if (a, g) == (0, 1):
+                grouped = held([P, PACK * W], BF16, "w1_bf01", tag="media_bf3")
+            else:
+                grouped = stage_tile(f"w1_bf{a}{g}", PACK * W, (a, g) == (1, 1))
             copy_on(
                 engine,
                 grouped[:].rearrange("p (t b i j) -> p b t j i", t=4, i=4, j=4),
@@ -160,7 +166,7 @@ def tile_list_vaccine_uptake_step_kernel(
             copy_on(
                 engine,
                 grouped[:].rearrange("p (c i j) -> p c j i", i=4, j=4),
-                media_raw[m][:].rearrange("p j (c i) -> p c j i", i=4),
+                media_raw[m].rearrange("p j (c i) -> p c j i", i=4),
             )
             media_q[m] = quantize(grouped, f"media_{m}")
 
@@ -187,8 +193,8 @@ def tile_list_vaccine_uptake_step_kernel(
         b_late = {2: (2, "media_raw2"), 5: (3, "w1_raw11")}
         late = {}
 
-        a_banks = [[0, 1, 6, 7, 2, 3, 6, 7], [2, 3, 6, 7, 1, 5, 4, 0]]
-        b_banks = [[2, 3, 6, 7, 0, 1, 0, 1], [4, 5, 2, 3, 4, 5, 4, 0]]
+        a_banks = [[0, 1, 6, 7, 0, 1, 4, 5], [0, 1, 6, 4, 5, 7, 2, 3]]
+        b_banks = [[2, 3, 6, 7, 4, 5, 6, 7], [4, 5, 2, 3, 6, 7, 2, 3]]
 
         def bank(shape, name, number):
             return psum.tile(shape, F32, name=name, offset=4 * W * number)
@@ -218,7 +224,7 @@ def tile_list_vaccine_uptake_step_kernel(
                     b_sb[g, jb] = ring.tile([P, JB, PACK], F32, name=f"b_sb{g}{jb}", tag="b_sb", bufs=B_RING)[:]
                 nc.scalar.copy(b_sb[g, jb], b_bank[:].rearrange("p t n -> p n t"))
 
-        h_tiles = {(0, 0): (2, "media_bf1"), (0, 2): (2, "media_bf2"), (0, 4): (4, "media_bf3")}
+        h_tiles = {(0, 0): (4, "media_bf1"), (0, 4): (4, "table1")}
         h_tiles.update({(1, 0): (4, "media_raw0"), (1, 4): (4, "media_raw1")})
 
         def make_h(g, blocks):
@@ -248,7 +254,7 @@ def tile_list_vaccine_uptake_step_kernel(
                     ALU.max,
                 )
 
-        h_tag = {(0, 0): "w1_raw01", (0, 1): "w1_bf11", (1, 0): "", (1, 1): "w3_bf1"}
+        h_tag = {(0, 0): "media_bf2", (0, 1): "w1_bf11", (1, 0): "", (1, 1): "w3_bf1"}
 
         def quantize_h(g, half):
             codes = held([P, W], U32, f"h_{g}{half}_codes", tag=h_tag[g, half])
@@ -280,15 +286,15 @@ def tile_list_vaccine_uptake_step_kernel(
         make_h(0, [0, 1])
         make_b(0, 1)
         gather_state(0)
-        prep_media(2, "scalar")
         make_h(0, [2, 3])
-        make_b(1, 1)
-        make_b(0, 2)
+        prep_media(2, "scalar")
         quantize_h(0, 0)
-        prep_w1(0, 1, "vector")
         prep_media(3, "scalar")
-        make_h(0, [4, 5])
+        make_b(0, 2)
         make_b(0, 3)
+        make_b(1, 1)
+        prep_w1(0, 1, "vector")
+        make_h(0, [4, 5])
         make_b(1, 2)
         gather_state(1)
         make_h(0, [6, 7])

@@ -154,11 +154,16 @@ def tile_list_vaccine_uptake_step_kernel(
                 grouped = held([P, PACK * W], BF16, "w1_bf01", tag="media_bf3")
             else:
                 grouped = stage_tile(f"w1_bf{a}{g}", PACK * W, (a, g) == (1, 1))
+            shared = PACK - 1 if (a, g) == (1, 1) else PACK
             copy_on(
                 engine,
-                grouped[:].rearrange("p (t b i j) -> p b t j i", t=4, i=4, j=4),
-                w1_raw[a, g][:].rearrange("p j (b t i) -> p b t j i", t=4, i=4),
+                grouped[:].rearrange("p (t b i j) -> p b t j i", t=4, i=4, j=4)[:, :, :shared],
+                w1_raw[a, g][:].rearrange("p j (b t i) -> p b t j i", t=4, i=4)[:, :, :shared],
             )
+            if shared < PACK:
+                rows = w1_raw[a, g][:].rearrange("p j (b t i) -> p t b i j", t=4, i=4)
+                words = grouped[:].rearrange("p (t b i j) -> p t b i j", t=4, i=4, j=4)
+                nc.gpsimd.tensor_scalar(words[:, shared], rows[:, shared], 1.0, 0.0, ALU.mult, ALU.add)
             w1_q[a, g] = quantize(grouped, f"w1_{a}{g}")
 
         def prep_media(m, engine):

from contextlib import ExitStack

import concourse.mybir as mybir

T, S, K, M, H, N = 2048, 1024, 1024, 512, 1024, 512
FLOPS = 2 * S * H * (K + M + N)

F32 = mybir.dt.float32
BF16 = mybir.dt.bfloat16
I32 = mybir.dt.int32
U32 = mybir.dt.uint32
U16 = mybir.dt.uint16
U8 = mybir.dt.uint8
FP8X4 = mybir.dt.float8_e4m3fn_x4
FP4X4 = mybir.dt.float4_e2m1fn_x4
ACT = mybir.ActivationFunctionType
ALU = mybir.AluOpType

P = 128
PACK = 4
W = 512
JB = 128
MEDIA_CUTS = [0, 256, 512, 768, 1024]
B_RING = 9


def tile_list_vaccine_uptake_step_kernel(
    tc, tab_words, tab_scales, offs, w1, media, wm4_words, wm4_scales, w3, goal, gT, out_0, out_1, out_2
):
    nc = tc.nc
    with ExitStack() as ctx:
        keep = ctx.enter_context(tc.tile_pool(name="keep", bufs=1))
        ring = ctx.enter_context(tc.tile_pool(name="ring", bufs=1))
        psum = ctx.enter_context(tc.psum_pool(name="psum", bufs=1))

        def held(shape, dtype, name, tag=""):
            return keep.tile(shape, dtype, name=name, tag=tag or name, align_bytes=64)

        table, w1_raw, media_raw, w3_raw, page = {}, {}, {}, {}, {}
        picked, w1_q, media_q, w3_q, h_q, h_bf, state, b_sb = {}, {}, {}, {}, {}, {}, {}, {}

        def load_table(a):
            table[a] = held([P, T], I32, f"table{a}")
            nc.sync.dma_start(table[a][:], tab_words[a].rearrange("p t i -> p (t i)").bitcast(I32))

        def load_rows(src, name):
            raw = held([P, PACK, src.shape[1]], F32, name)
            nc.sync.dma_start(raw[:], src.rearrange("(p j) c -> p j c", j=PACK))
            return raw

        def load_w1(a, g):
            w1_raw[a, g] = load_rows(w1[W * a : W * (a + 1), W * g : W * (g + 1)], f"w1_raw{a}{g}")

        def load_media(m):
            if m < 2:
                media_raw[m] = load_rows(media[:, MEDIA_CUTS[m] : MEDIA_CUTS[m + 1]], f"media_raw{m}")[:]
            else:
                both = load_rows(media[:, W:], "media_raw2")
                media_raw[2], media_raw[3] = both[:, :, : W // 2], both[:, :, W // 2 :]

        def load_w3(g):
            w3_raw[g] = held([P, PACK, W], F32, f"w3_raw{g}")
            rows = w3[W * g : W * (g + 1), :].rearrange("(b t i) n -> t b i n", t=PACK, i=4)
            for t in range(PACK):
                nc.sync.dma_start(w3_raw[g][:, t, :], rows[t])

        def load_page(t):
            page[t] = held([P, T], F32, f"page{t}")
            nc.sync.dma_start(page[t][:], gT.rearrange("(p t) c -> t p c", t=PACK)[t])

        offsets = keep.tile([P, S // 16], U16, name="offsets")
        nc.sync.dma_start(offsets[:], offs)
        tab_plane = held([P, T], U8, "tab_plane")
        nc.sync.dma_start(tab_plane[0:32, :].bitcast(I32), tab_scales.rearrange("a q t -> (a q) t").bitcast(I32))
        wm_plane_raw = held([P, H], U8, "wm_plane_raw")
        nc.gpsimd.memset(tab_plane[32:64, :].bitcast(I32), 0)
        nc.gpsimd.memset(tab_plane[64:P, :].bitcast(I32), 0)
        nc.gpsimd.memset(wm_plane_raw[:].bitcast(I32), 0)
        picked_rows = held([P, S], U8, "picked_rows")
        nc.vector.tensor_copy(picked_rows[:], tab_plane[:].indirect(offsets[:]))
        picked_plane = [held([P, S], U8, f"picked_plane{a}") for a in range(2)]
        for plane in picked_plane:
            nc.gpsimd.memset(plane[:].bitcast(I32), 0)

        def move_rows(a, r):
            nc.sync.dma_start(
                picked_plane[a][4 * a + r : P : 32, :].bitcast(I32),
                picked_rows[16 * a + r : 16 * a + 16 : 4, :].bitcast(I32),
            )

        wm_rows = wm4_scales[0].rearrange("(q r) c -> r q c", r=4)

        def load_wm_rows(r):
            nc.sync.dma_start(wm_plane_raw[r:P:32, :].bitcast(I32), wm_rows[r].bitcast(I32))

        load_table(0)
        wm_raw = held([P, H // 2], I32, "wm_raw")
        nc.sync.dma_start(wm_raw[:], wm4_words[0].bitcast(I32))
        load_wm_rows(0)
        load_wm_rows(1)
        load_media(0)
        load_wm_rows(2)
        load_wm_rows(3)
        load_w1(0, 0)
        move_rows(0, 0)
        move_rows(0, 1)
        move_rows(0, 2)
        load_w1(1, 0)
        move_rows(0, 3)
        move_rows(1, 0)
        load_table(1)
        move_rows(1, 1)
        move_rows(1, 2)
        move_rows(1, 3)
        load_media(1)
        load_page(0)
        load_media(2)
        load_w1(0, 1)
        load_page(1)
        load_w1(1, 1)
        load_w3(0)
        load_w3(1)
        goal_sb = held([P, PACK], F32, "goal_sb")
        nc.sync.dma_start(goal_sb[:], goal.rearrange("(p t) -> p t", t=PACK))
        load_page(2)
        load_page(3)

        warm = held([P, 8], F32, "warm")
        nc.gpsimd.memset(warm[:], 0.0)
        nc.scalar.activation(warm[:], warm[:], ACT.Sigmoid)
        neg_goal = held([P, PACK], F32, "neg_goal")
        nc.scalar.mul(neg_goal[:], goal_sb[:], -1.0)

        def copy_on(engine, out, in_):
            if engine == "vector":
                nc.vector.tensor_copy(out, in_)
            else:
                nc.scalar.copy(out, in_)

        def quantize(grouped, name, tag=""):
            width = grouped.shape[1] // PACK
            codes = held([P, width], U32, name + "_codes", tag=tag)
            plane = held([P, width], U8, name + "_plane")
            nc.vector.quantize_mx(out=codes[:].bitcast(FP8X4), scales=plane[:], in_=grouped[:])
            return codes, plane

        def stage_tile(name, width, own):
            if own:
                return held([P, width], BF16, name)
            return ring.tile([P, width], BF16, name=name, tag="stage", bufs=2, align_bytes=64)

        def prep_w1(a, g, engine):
            if (a, g) == (0, 1):
                grouped = held([P, PACK * W], BF16, "w1_bf01", tag="media_bf3")
            else:
                grouped = stage_tile(f"w1_bf{a}{g}", PACK * W, (a, g) == (1, 1))
            shared = PACK - 1 if (a, g) == (1, 1) else PACK
            copy_on(
                engine,
                grouped[:].rearrange("p (t b i j) -> p b t j i", t=4, i=4, j=4)[:, :, :shared],
                w1_raw[a, g][:].rearrange("p j (b t i) -> p b t j i", t=4, i=4)[:, :, :shared],
            )
            if shared < PACK:
                rows = w1_raw[a, g][:].rearrange("p j (b t i) -> p t b i j", t=4, i=4)
                words = grouped[:].rearrange("p (t b i j) -> p t b i j", t=4, i=4, j=4)
                nc.gpsimd.tensor_scalar(words[:, shared], rows[:, shared], 1.0, 0.0, ALU.mult, ALU.add)
            w1_q[a, g] = quantize(grouped, f"w1_{a}{g}")

        def prep_media(m, engine):
            grouped = stage_tile(f"media_bf{m}", PACK * (MEDIA_CUTS[m + 1] - MEDIA_CUTS[m]), m >= 1)
            copy_on(
                engine,
                grouped[:].rearrange("p (c i j) -> p c j i", i=4, j=4),
                media_raw[m].rearrange("p j (c i) -> p c j i", i=4),
            )
            media_q[m] = quantize(grouped, f"media_{m}")

        def prep_w3(g, engine):
            grouped = stage_tile(f"w3_bf{g}", PACK * W, g == 1)
            copy_on(
                engine,
                grouped[:].rearrange("p (t m j) -> p m j t", t=4, j=4),
                w3_raw[g][:].rearrange("p j (m t) -> p m j t", t=4),
            )
            w3_q[g] = quantize(grouped, f"w3_{g}")

        def gather_words(a, cuts):
            picked[a] = held([P, S], U32, f"picked{a}")
            for lo, hi in zip(cuts, cuts[1:]):
                nc.vector.tensor_copy(picked[a][:, lo:hi], table[a][:].bitcast(U32).indirect(offsets[:, lo // 16 : hi // 16]))

        state_tag = ["state0", "state1", "media_raw1", "w1_raw00"]

        def gather_state(t):
            state[t] = held([P, S], F32, f"state{t}", tag=state_tag[t])
            nc.vector.tensor_copy(state[t][:], page[t][:].indirect(offsets[:]))

        b_late = {2: (2, "media_raw2"), 5: (3, "w1_raw11")}
        late = {}

        a_banks = [[0, 1, 6, 7, 0, 1, 4, 5], [0, 1, 6, 4, 5, 7, 2, 3]]
        b_banks = [[2, 3, 6, 7, 4, 5, 6, 7], [4, 5, 2, 3, 6, 7, 2, 3]]

        def bank(shape, name, number):
            return psum.tile(shape, F32, name=name, offset=4 * W * number)

        def make_b(g, m):
            for jb in range(MEDIA_CUTS[m] // JB, MEDIA_CUTS[m + 1] // JB):
                local = slice(JB * jb - MEDIA_CUTS[m], JB * (jb + 1) - MEDIA_CUTS[m])
                b_bank = bank([P, PACK, JB], f"b_bank{g}{jb}", b_banks[g][jb])
                for t in range(PACK):
                    r0 = W * g + P * t
                    nc.tensor.matmul_mx(
                        out=b_bank[:, t, :],
                        lhsT=wm_codes[:].bitcast(U8)[:, 2 * r0 : 2 * (r0 + P)].bitcast(FP4X4),
                        lhsT_scale=wm_plane[:, r0 : r0 + P],
                        rhs=media_q[m][0][:, local].bitcast(FP8X4),
                        rhs_scale=media_q[m][1][:, local],
                        start=True,
                        stop=True,
                    )
                if g == 1 and jb in b_late:
                    count, tag = b_late[jb]
                    shared = held([P, count, JB, PACK], F32, f"b_late{jb}", tag=tag)
                    late.update({jb + n: shared[:, n] for n in range(count)})
                if g == 1 and jb in late:
                    b_sb[g, jb] = late[jb]
                else:
                    b_sb[g, jb] = ring.tile([P, JB, PACK], F32, name=f"b_sb{g}{jb}", tag="b_sb", bufs=B_RING)[:]
                nc.scalar.copy(b_sb[g, jb], b_bank[:].rearrange("p t n -> p n t"))

        h_tiles = {(0, 0): (4, "media_bf1"), (0, 4): (4, "table1")}
        h_tiles.update({(1, 0): (4, "media_raw0"), (1, 4): (4, "media_raw1")})

        def make_h(g, blocks):
            for jb in blocks:
                first = max(f for gg, f in h_tiles if gg == g and f <= jb)
                local = jb - first
                if local == 0:
                    count, tag = h_tiles[g, first]
                    h_bf[g, first] = held([P, PACK * JB * count], BF16, f"h_bf{g}{first}", tag=tag)
                cols = slice(JB * jb, JB * (jb + 1))
                a_bank = bank([P, PACK, JB], f"a_bank{g}{jb}", a_banks[g][jb])
                for a in range(2):
                    for t in range(PACK):
                        nc.tensor.matmul_mx(
                            out=a_bank[:, t, :],
                            lhsT=w1_q[a, g][0][:, P * t : P * (t + 1)].bitcast(FP8X4),
                            lhsT_scale=w1_q[a, g][1][:, P * t : P * (t + 1)],
                            rhs=picked[a][:, cols].bitcast(FP8X4),
                            rhs_scale=picked_plane[a][4 * a : P, cols],
                            start=(a == 0 and t == 0),
                            stop=(a == 1 and t == PACK - 1),
                        )
                nc.vector.tensor_tensor(
                    h_bf[g, first][:, PACK * JB * local : PACK * JB * (local + 1)].rearrange("p (n t) -> p n t", t=PACK),
                    a_bank[:].rearrange("p t n -> p n t"),
                    b_sb[g, jb],
                    ALU.max,
                )

        h_tag = {(0, 0): "media_bf2", (0, 1): "w1_bf11", (1, 0): "", (1, 1): "w3_bf1"}

        def quantize_h(g, half):
            codes = held([P, W], U32, f"h_{g}{half}_codes", tag=h_tag[g, half])
            plane = held([P, W], U8, f"h_{g}{half}_plane")
            for (gg, first), (count, tag) in h_tiles.items():
                if gg == g and first * JB // W == half:
                    cols = slice(first * JB - W * half, (first + count) * JB - W * half)
                    nc.vector.quantize_mx(out=codes[:, cols].bitcast(FP8X4), scales=plane[:, cols], in_=h_bf[g, first][:])
            h_q[g, half] = codes, plane

        gather_words(0, [0, S])
        wm_codes = held([P, H // 2], I32, "wm_codes")
        nc.vector.tensor_copy(
            wm_codes[:].rearrange("p (g t b w) -> p g b t w", g=2, t=4, w=2),
            wm_raw[:].rearrange("p (g b t w) -> p g b t w", g=2, t=4, w=2),
        )
        prep_media(0, "scalar")
        wm_plane = held([P, H], U8, "wm_plane")
        nc.vector.tensor_copy(
            wm_plane[:].bitcast(I32).rearrange("p (g t b) -> p g b t", g=2, t=4),
            wm_plane_raw[:].bitcast(I32).rearrange("p (g b t) -> p g b t", g=2, t=4),
        )
        prep_w1(0, 0, "vector")
        make_b(0, 0)
        prep_w1(1, 0, "vector")
        make_b(1, 0)
        gather_words(1, [0, 256, S])
        prep_media(1, "scalar")
        make_h(0, [0, 1])
        make_b(0, 1)
        gather_state(0)
        make_h(0, [2, 3])
        prep_media(2, "scalar")
        quantize_h(0, 0)
        prep_media(3, "scalar")
        make_b(0, 2)
        make_b(0, 3)
        make_b(1, 1)
        prep_w1(0, 1, "vector")
        make_h(0, [4, 5])
        make_b(1, 2)
        gather_state(1)
        make_h(0, [6, 7])
        prep_w1(1, 1, "scalar")
        quantize_h(0, 1)
        prep_w3(0, "scalar")
        make_b(1, 3)
        make_h(1, range(S // JB))
        prep_w3(1, "scalar")
        quantize_h(1, 0)
        quantize_h(1, 1)

        reuse = ["w1_raw00", "w1_raw10", "w1_raw01", "w1_raw11"]
        blend = [held([P, S], F32, f"blend{t}", tag=reuse[t])[:] for t in range(PACK)]
        factor_pair = [held([P, 2, S], F32, f"factor_pair{u}", tag=f"w3_raw{1 - u}") for u in range(2)]
        factor = [factor_pair[t // 2][:, t % 2, :] for t in range(PACK)]

        def make_factor(t):
            nc.scalar.activation(
                factor[t], state[t][:], ACT.Identity, bias=goal_sb[:, t : t + 1], scale=neg_goal[:, t : t + 1]
            )

        make_factor(0)
        for t in range(PACK):
            for half in range(2):
                e_bank = bank([P, W], f"e_bank{t}{half}", a_banks[1][2 * t + half])
                for g in range(2):
                    nc.tensor.matmul_mx(
                        out=e_bank[:],
                        lhsT=w3_q[g][0][:, P * t : P * (t + 1)].bitcast(FP8X4),
                        lhsT_scale=w3_q[g][1][:, P * t : P * (t + 1)],
                        rhs=h_q[g, half][0][:].bitcast(FP8X4),
                        rhs_scale=h_q[g, half][1][:],
                        start=(g == 0),
                        stop=(g == 1),
                    )
                nc.scalar.activation(blend[t][:, W * half : W * (half + 1)], e_bank[:], ACT.Sigmoid)
        make_factor(1)
        gather_state(2)
        make_factor(2)

        half_t = T // 2
        y_bf = [held([P, half_t, PACK], BF16, f"y_bf{c}", tag=["w3_bf1", "w3_1_codes"][c]) for c in range(2)]
        y_rows = out_0.rearrange("(p t) c -> t p c", t=PACK)
        for t in range(PACK):
            nc.vector.tensor_tensor(page[t][:].indirect(offsets[:]), blend[t], factor[t], ALU.mult)
            nc.sync.dma_start(y_rows[t], page[t][:])
            if t < PACK - 1:
                for c in range(2):
                    piece = page[t][:, half_t * c : half_t * (c + 1)]
                    if t == PACK - 2 and c == 0:
                        nc.scalar.copy(y_bf[c][:, :, t : t + 2], piece.unsqueeze(2).to_broadcast([P, half_t, 2]))
                    else:
                        nc.scalar.copy(y_bf[c][:, :, t], piece)
            if t == 1:
                gather_state(PACK - 1)
                make_factor(PACK - 1)
        last = PACK - 1
        y_plane = held([P, T], U8, "y_plane")
        y_codes = held([P, T], I32, "y_codes", tag="table0")
        y_words = out_1[0].rearrange("p m t -> p (m t)").bitcast(I32)
        for x in range(0, half_t, W):
            nc.vector.tensor_copy(y_bf[0][:, x : x + W, last], page[last][:, x : x + W])
        for x in range(0, half_t, W):
            nc.scalar.copy(y_bf[1][:, x : x + W, last], page[last][:, half_t + x : half_t + x + W])
        for x in range(0, T, W):
            lo = x % half_t
            nc.vector.quantize_mx(
                out=y_codes[:, x : x + W].bitcast(FP8X4),
                scales=y_plane[:, x : x + W],
                in_=y_bf[x // half_t][:, lo : lo + W, :].rearrange("p c t -> p (c t)"),
            )
            nc.sync.dma_start(y_words[:, x : x + W], y_codes[:, x : x + W])
        y_scales = out_2[0].rearrange("(q r) m -> r q m", r=4)
        for r in range(4):
            queue = nc.sync if r % 2 == 0 else nc.scalar
            queue.dma_start(y_scales[r].bitcast(I32), y_plane[r:P:32, :].bitcast(I32))
